import numpy as np, ml_dtypes
CORES = [23,119,17,113]
N = 4
BF = ml_dtypes.bfloat16
W, S, B, M = 8192, 768, 8, 5
def dot(a, x):
    return np.add.reduce(a[:, :, None] * x, axis=1)
def put(w, a, x):
    z = B * np.arange(S) + (dot(a, x) & (B - 1))
    np.put_along_axis(w, z[:, None, :], x, 2)
def pack(b, e, q):
    return {"tab": b.reshape(N, 128, W).astype(np.float32).astype(BF), "res": e.reshape(N, 128, M * S).astype(np.float32).astype(BF), "hw": q.reshape(N, 128, 3).astype(np.float32).astype(BF)}
def parts(rng):
    return rng.integers(0, 256, (N, 8, 16, W)), rng.integers(0, 256, (N, 8, 16, M, S)), rng.integers(0, 256, (N, 8, 16, 3))
def store(b, x, q):
    e = np.array(x)
    for r in range(N):
        w = np.array(b[r])
        for t in range(M):
            if t > 0:
                h = dot(q[r, :, :, 0], x[r, :, :, t - 1])
                if r > 0: h = h + dot(q[r - 1, :, :, 1], x[r - 1, :, :, t])
                e[r, :, :, t] = (x[r, :, :, t] - np.take_along_axis(w, (h & (W - 1))[:, None, :], 2)) & 255
            put(w, q[r, :, :, 2], x[r, :, :, t])
    return e
def plant(rng, goal, code):
    b, x, q = parts(rng)
    q[:, :, 0, 0] = 1; q[:, :, 1, 0] = 128; q[:, :, :2, 2] = 16 * rng.integers(0, 16, (N, 8, 2)); q[:, :, 2, 2] = 1
    for r in range(N):
        for t in range(M):
            rest = dot(q[r, :, 3:, 2], x[r, :, 3:, t])
            x[r, :, 2, t] = B * rng.integers(0, 256 // B, (8, S)) + ((code[r, :, t] - rest) & (B - 1))
            if t + 1 < M:
                d = goal[r, :, t + 1] - dot(q[r, :, 2:, 0], x[r, :, 2:, t])
                if r > 0: d = d - dot(q[r - 1, :, :, 1], x[r - 1, :, :, t + 1])
                d = d & (W - 1); x[r, :, 0, t] = d & 127; x[r, :, 1, t] = d >> 7
    return pack(b, store(b, x, q), q)
def chase(rng, code, lag):
    o = rng.integers(0, S, code.shape); t = np.maximum(np.arange(M)[None, None, :, None] - lag, 0)
    return B * o + code[np.arange(N)[:, None, None, None], np.arange(8)[None, :, None, None], t, o]
def setup_inputs(rng):
    return pack(*parts(rng))
def setup_inputs_fresh(rng):
    code = rng.integers(0, B, (N, 8, M, S)); code = np.where(rng.random((N, 8, 1, S)) < 0.5, code[:, :, :1], code)
    a = rng.permutation(N)[:2]; t = np.arange(M)[None, :, None]
    code[a] = (rng.integers(0, B, (2, 8, 1, S)) + t[None] * (1 + 2 * rng.integers(0, B // 2, (2, 8, 1, S)))) & (B - 1)
    goal = chase(rng, code, rng.integers(1, M, code.shape)); goal[:, ::4, 1:] = B * np.arange(S) + code[:, ::4, :-1]
    goal = np.where(rng.random(code.shape) < 0.1, rng.integers(0, W, code.shape), goal)
    one = np.maximum(t - 1, 0) + np.zeros((8, M, S), np.int64)
    two = np.floor(rng.random((8, M, S)) * np.maximum(t - 1, 1)).astype(np.int64)
    for i, came in ((0, one), (1, two)):
        o = np.argsort(rng.random((8, M, S)), axis=-1)
        goal[a[i]] = B * o + code[a[i]][np.arange(8)[:, None, None], came, o]
    return plant(rng, goal, code)
def setup_inputs_same(rng):
    code = (rng.integers(0, B, (N, 8, 1, S)) + np.arange(M)[None, None, :, None] * rng.integers(1, B, (N, 8, 1, S))) & (B - 1)
    return plant(rng, chase(rng, code, rng.integers(0, 2, code.shape)), code)
def setup_inputs_alike(rng):
    goal = rng.integers(0, W, (N, 8, M, S)); code = rng.integers(0, B, (N, 8, M, S)); p = rng.permutation(8); last = S * B - 1
    goal[:, p[0]] = 0; goal[:, p[1]] = W - 1; goal[:, p[2]] = last; goal[:, p[3]] = S * B if S * B < W else W // 2
    goal[:, p[4]] = np.argsort(rng.random((N, M, W)), axis=-1)[..., :S]
    goal[:, p[5]] = rng.choice(np.array([0, B - 1, B, last]), (N, M, S))
    goal[:, p[6]] = B * np.arange(S) + rng.integers(0, B, (N, M, S))
    code[:, p[0]] = 0; code[:, p[2]] = B - 1; code[:, p[5]] = code[:, p[5], :1]
    goal[rng.integers(0, N)] = (W // 4) * rng.integers(0, 4, (1, M, 1)) + np.argsort(rng.random((8, M, W // 4)), axis=-1)[..., :S]
    return plant(rng, goal, code)
def setup_inputs_ends(rng):
    b, x, q = parts(rng); p = rng.permutation(8)
    q[:, p[0], :, 0] = 0; q[:, p[1], :, 1] = 0; q[:, p[2]] = 255; x[:, p[2]] = 255; q[:, p[3], :, 2] = 0; q[:, p[4]] = 0
    q[:, p[3], :, :2] = rng.integers(200, 256, (N, 16, 2))
    x[:, p[3]] = 255 - np.floor(rng.random((N, 16, M, S)) * rng.integers(56, 257, (N, 1, M, S))).astype(np.int64)
    x[:, p[5]] = 255 * rng.integers(0, 2, (N, 16, M, S))
    b[:, p[6]] = 255; x[:, p[6]] = rng.choice(np.array([0, 1, 254, 255]), (N, 16, M, S))
    x[:, p[7]] = x[:, p[7]] * (rng.random((N, 16, M, S)) < 0.1); q[:, p[7]] = rng.choice(np.array([0, 1, 128, 255]), (N, 16, 3))
    return pack(b, store(b, x, q), q)
def uneven(rng, *shape):
    return np.floor(rng.random(shape) * np.exp2(rng.integers(0, 9, (N, 8, 1) + shape[3:]))).astype(np.int64)
def setup_inputs_spread(rng):
    q = np.floor(rng.random((N, 8, 16, 3)) * np.exp2(rng.integers(0, 9, (N, 8, 16, 3)))).astype(np.int64)
    return pack(uneven(rng, N, 8, 16, W), uneven(rng, N, 8, 16, M, S), q)
def check_inputs(d):
    bad = []
    for k in ("tab", "res", "hw"):
        a = np.asarray(d[k]).astype(np.float32)
        if not np.all((a >= 0) & (a <= 255) & (a == np.floor(a))): bad.append("whole numbers from 0 to 255 in " + k)
    return bad
def reference(tab, res, hw):
    b = tab.astype(np.float32).astype(np.int64).reshape(N, 8, 16, W)
    e = res.astype(np.float32).astype(np.int64).reshape(N, 8, 16, M, S)
    q = hw.astype(np.float32).astype(np.int64).reshape(N, 8, 16, 3)
    y = np.zeros((N, 8, 16, M, S), np.int64)
    for r in range(N):
        w = np.array(b[r])
        for t in range(M):
            x = e[r, :, :, t]
            if t > 0:
                h = dot(q[r, :, :, 0], y[r, :, :, t - 1])
                if r > 0: h = h + dot(q[r - 1, :, :, 1], y[r - 1, :, :, t])
                x = (np.take_along_axis(w, (h & (W - 1))[:, None, :], 2) + x) & 255
            y[r, :, :, t] = x
            put(w, q[r, :, :, 2], x)
    return {"y": y.reshape(N, 128, M * S).astype(np.float32).astype(BF)}

@@ -1,0 +1,422 @@
+from concourse.mybir import AluOpType, ActivationFunctionType
+
+W, S, M = 8192, 768, 5
+H = S // 2
+C = H // 16
+Q = 6
+PA = 3
+TW = 2
+NP = 4
+
+SCRATCH = {
+    "tb": ("sbuf", [128, W], "bfloat16"),
+    "er": ("sbuf", [128, M * S], "bfloat16"),
+    "ep": ("sbuf", [128, 4 * S], "bfloat16"),
+    "sp": ("sbuf", [128, 4 * S], "bfloat16"),
+    "sg": ("sbuf", [128, 4 * S], "bfloat16"),
+    "xs": ("sbuf", [128, 4 * S], "bfloat16"),
+    "mm": ("sbuf", [128, H], "bfloat16"),
+    "hws": ("sbuf", [128, 16], "bfloat16"),
+    "Ls": ("sbuf", [128, 2, 160], "bfloat16"),
+    "Lg": ("sbuf", [128, 2, 160], "bfloat16"),
+    "Lh": ("sbuf", [128, 2, 160], "bfloat16"),
+    "Gp": ("sbuf", [128, 2, 4], "bfloat16"),
+    "one8": ("sbuf", [128, 2, 4], "bfloat16"),
+    "ones": ("sbuf", [128, 128], "bfloat16"),
+    "negs": ("sbuf", [128, 128], "bfloat16"),
+    "negh": ("sbuf", [128, 128], "bfloat16"),
+    "idp": ("sbuf", [128, 128], "bfloat16"),
+    "idn": ("sbuf", [128, 128], "bfloat16"),
+    "idh": ("sbuf", [128, 128], "bfloat16"),
+    "c128": ("sbuf", [128, 16], "bfloat16"),
+    "pint": ("sbuf", [128, 8], "int32"),
+    "mint": ("sbuf", [128, 8], "int32"),
+    "mflt": ("sbuf", [128, 8], "float32"),
+    "c16": ("sbuf", [128, 2, C], "float32"),
+    "jj": ("sbuf", [128, 2, C], "float32"),
+    "Tt": ("sbuf", [128, 2 * M, 128], "float32"),
+    "Tc": ("sbuf", [128, 32], "float32"),
+    "cvin": ("sbuf", [128, 8], "float32"),
+    "bias2": ("sbuf", [128, 8], "float32"),
+    "land": ("sbuf", [128, 8, C], "float32"),
+    "hu": ("sbuf", [128, 8, C], "float32"),
+    "hi": ("sbuf", [128, 8, C], "int32"),
+    "hj": ("sbuf", [128, 8, C], "int32"),
+    "offu": ("sbuf", [128, 8, C], "uint16"),
+    "qw": ("sbuf", [128, 8, C], "int32"),
+    "fw": ("sbuf", [128, 8, C], "float32"),
+    "offw": ("sbuf", [128, 8, C], "uint16"),
+    "R0": ("psum", [128, 2, 512], "float32"),
+    "R1": ("psum", [128, 2, 512], "float32"),
+    "RC": ("psum", [128, 2, 512], "float32"),
+    "X0": ("psum", [128, 512], "float32"),
+    "X1": ("psum", [128, 512], "float32"),
+}
+SEMAPHORES = (
+    ["d_hw", "d_e0", "d_e1", "d_e2", "d_e3", "d_e4", "d_t0", "d_t1", "d_t2", "d_y"]
+    + ["v_one8", "v_z", "v_ones", "v_c128", "v_m0", "v_m1", "v_jj", "v_ls", "v_lg", "v_tc"]
+    + ["g_g0", "g_g1", "g_pi", "g_c16", "g_id"]
+    + ["p_c", "p_h0", "p_h1", "p_x0", "p_x1"]
+    + ["a_b2", "a_hu", "a_e0", "a_e1", "a_s00", "a_s01", "a_s10", "a_s11", "a_x0", "a_x1"]
+    + ["v_g00", "v_g01", "v_g10", "v_g11", "v_t0", "v_t1", "v_ua", "v_ub", "v_uc", "v_wa", "v_wb", "v_wc",
+       "v_s", "v_m", "v_x"]
+    + ["r_c", "l_c"] + ["r_b%d" % i for i in range(8)] + ["l_%d" % t for t in range(1, M)]
+)
+
+
+def rank_program(g, core, T, topo):
+    rank = T.rank_of(core)
+    if rank is None:
+        return
+    n = len(T.cores)
+    first, last = rank == 0, rank == n - 1
+    V, A, P, D = g.vector, g.scalar, g.tensor, g.sync
+    add, sub, mul = AluOpType.add, AluOpType.subtract, AluOpType.mult
+    IDENT, SIGN = ActivationFunctionType.Identity, ActivationFunctionType.Sign
+    cnt, seen, done = {}, {}, {}
+
+    def sig(ins, name, k=1):
+        ins.then_inc(T.sem[name], k)
+        return owe(name, k)
+
+    def owe(name, k):
+        cnt[name] = cnt.get(name, 0) + k
+        return (name, cnt[name])
+
+    def wait(qn, *toks):
+        q = {"V": V, "A": A, "P": P, "D": D, "g": g}[qn]
+        for tok in toks:
+            if tok is None or seen.get((qn, tok[0]), 0) >= tok[1]:
+                continue
+            q.wait_ge(T.sem[tok[0]], tok[1])
+            seen[(qn, tok[0])] = tok[1]
+            done[tok[0]] = max(done.get(tok[0], 0), tok[1])
+
+    if not last:
+        nxt = T.cores[rank + 1]
+        rid, pid, _ = topo.addr(nxt)
+        omask, oeng = topo.mask(core, nxt), len(topo.engines(core, nxt))
+    if not first:
+        ieng = len(topo.engines(T.cores[rank - 1], core))
+
+    def send(dst, src, rsem, lsem):
+        g.remote_dma(dst, src, T.sem[rsem], T.sem[lsem], pid, rid, omask)
+        return owe(lsem, oeng)
+
+    d_hw = sig(A.dma_start(T.hws[:, 0:3], T.hw[:]), "d_hw", 16)
+    d_e = {}
+
+    def load_e(t0, t1):
+        tok = sig(D.dma_start(T.er[:, t0 * S:t1 * S], T.res[:, t0 * S:t1 * S]), "d_e%d" % t0, 16)
+        for t in range(t0, t1):
+            d_e[t] = tok
+
+    def load_t(i, a, b):
+        return sig(D.dma_start(T.tb[:, a:b], T.tab[:, a:b]), "d_t%d" % i, 16)
+
+    load_e(0, 1)
+    d_t = [load_t(0, 0, 8 * H), load_t(1, 8 * H, 8 * S)]
+    load_e(1, 2)
+    d_t.append(load_t(2, 8 * S, W))
+    load_e(2, 3 if first else M)
+
+    def store(a, b):
+        sig(D.dma_start(T.y[:, a:b], T.xs[:, a - S:b - S]), "d_y", 16)
+
+    def store0():
+        wait("D", d_e[0])
+        sig(D.dma_start(T.y[:, 0:S], T.er[:, 0:S]), "d_y", 16)
+
+    if not first:
+        store0()
+
+    v_one8 = sig(V.memset(T.one8[:], 1.0), "v_one8")
+    for L in (T.Ls, T.Lg, T.Lh):
+        v_z = sig(V.memset(L[:], 0.0), "v_z")
+    for b, c in ((T.ones, 1.0), (T.negs, -128.0), (T.negh, -256.0)):
+        v_ones = sig(V.memset(b[:], c), "v_ones")
+    v_c128 = sig(V.memset(T.c128[:], 128.0), "v_c128")
+    g_pi = sig(g.iota(T.pint[:, 0:1], [[0, 1]], 0, 1), "g_pi")
+    wait("g", v_one8)
+    g0 = sig(g.affine_select(T.Gp[:], T.one8[:], [[-16, 2], [-32, 4]], AluOpType.is_ge, 0.0, 0, 1), "g_g0")
+    sig(g.iota(T.c16[:, 0, :], [[0, NP], [16, C // NP]], 0, 0, allow_small_or_imprecise_dtypes=True), "g_c16")
+    g_c16 = sig(g.iota(T.c16[:, 1, :], [[16, C]], 0, 0, allow_small_or_imprecise_dtypes=True), "g_c16")
+    wait("g", g0)
+    g1 = sig(g.affine_select(T.Gp[:], T.Gp[:], [[16, 2], [32, 4]], AluOpType.is_ge, 0.0, 15, -1), "g_g1")
+    wait("g", v_ones)
+    for o, b in ((T.idp, T.ones), (T.idn, T.negs), (T.idh, T.negh)):
+        g_id = sig(g.affine_select(o[:], b[:], [[-1, 128]], AluOpType.is_equal, 0.0, 0, 1), "g_id")
+    wait("V", g_pi)
+    m0 = sig(V.tensor_scalar(T.mint[:, 0:1], T.pint[:, 0:1], 15, None, AluOpType.bitwise_and), "v_m0")
+    wait("V", m0)
+    m1 = sig(V.tensor_copy(T.mflt[:, 0:1], T.mint[:, 0:1]), "v_m1")
+    wait("V", m1, g_c16)
+    v_jj = sig(V.tensor_scalar(T.jj[:], T.c16[:], T.mflt[:, 0:1], 0.4375, add, add), "v_jj")
+    wait("V", v_z, g1, d_hw)
+    for kind, scale in ((2, 0.125), (0, 1.0), (1, 1.0)):
+        o = 5 + Q * kind
+        v_ls = sig(V.tensor_scalar(T.Ls[:, :, o:o + 128:32], T.Gp[:], T.hws[:, kind:kind + 1], scale, mul, mul), "v_ls")
+    for L, scale in ((T.Lg, -128.0), (T.Lh, -256.0)):
+        for kind in (0, 1):
+            o = 5 + Q * kind
+            v_lg = sig(V.tensor_scalar(L[:, :, o:o + 128:32], T.Gp[:], T.hws[:, kind:kind + 1], scale, mul, mul), "v_lg")
+
+    R = [T.R0, T.R1]
+    X = [T.X0, T.X1]
+
+    def sums(k, L, src, base, q0, q1, start, stop):
+        ins = None
+        for q in range(q0, q1):
+            for par in range(2):
+                ins = P.matmul(R[k][:, par, 0:64], L[:, par, 5 - q:133 - q], src[:, base + 64 * q:base + 64 * q + 64],
+                               start and q == q0, stop and q == q1 - 1)
+        return ins
+
+    def turn(t, k, tok):
+        wait("V", tok)
+        for b in range(4):
+            out = sig(V.transpose(T.Tt[:, 2 * t + k, b:128:4], R[k][:, :, 16 * b:16 * b + 16]), "v_t%d" % k)
+        return out
+
+    def w_ops(t, k0, k1, tok):
+        a, b = 2 * t + k0, 2 * t + k1
+        st = {}
+
+        def wa():
+            wait("V", v_jj, *tok)
+            st["a"] = sig(V.tensor_tensor(T.qw[:, a:b, :], T.Tt[:, a:b, 2 * C:3 * C], T.jj[:, k0:k1, :], sub), "v_wa")
+
+        def wb():
+            wait("V", st["a"])
+            st["b"] = sig(V.tensor_tensor(T.fw[:, a:b, :], T.Tt[:, a:b, 2 * C:3 * C], T.qw[:, a:b, :], sub), "v_wb")
+
+        def wc():
+            wait("V", st["b"])
+            st["c"] = sig(V.tensor_scalar(T.offw[:, a:b, :], T.fw[:, a:b, :], 8.0, None, mul), "v_wc")
+        return [wa, wb, wc], st
+
+    def u_ops(t, k0, k1, tok):
+        a, b = 2 * (t - 1) + k0, 2 * (t - 1) + k1
+        st = {}
+
+        def ua():
+            wait("V", *tok)
+            if not first:
+                ins = V.tensor_tensor(T.hi[:, a:b, :], T.hu[:, a:b, :], T.land[:, a:b, :], add)
+            elif t == 1:
+                ins = V.tensor_copy(T.hi[:, a:b, :], T.Tt[:, a:b, 0:C])
+            else:
+                ins = V.tensor_scalar(T.hi[:, a:b, :], T.Tt[:, a:b, 0:C], T.Tc[:, 0:1], None, add)
+            st["a"] = sig(ins, "v_ua")
+
+        def ub():
+            wait("V", st["a"])
+            st["b"] = sig(V.tensor_scalar(T.hj[:, a:b, :], T.hi[:, a:b, :], W - 1, None, AluOpType.bitwise_and), "v_ub")
+
+        def uc():
+            wait("V", st["b"])
+            st["c"] = sig(V.tensor_copy(T.offu[:, a:b, :], T.hj[:, a:b, :]), "v_uc")
+        return [ua, ub, uc], st
+
+    def scatter(t, k, src, base, i=0):
+        a, b = (0, C) if k else (i * C // NP, (i + 1) * C // NP)
+        win = T.tb[:, 8 * H * k + 128 * a:8 * H * k + 128 * b]
+        o = base + H * k
+        return sig(V.tensor_copy(win.indirect(T.offw[:, 2 * t + k, a:b]), src[:, o + 16 * a:o + 16 * b]), "v_s")
+
+    a_e = {}
+
+    def shift_e(t):
+        wait("A", d_e[t])
+        for k in range(2):
+            o = H * k
+            a_e[(t, k)] = sig(A.activation(T.ep[:, (t - 1) * S + o:(t - 1) * S + o + H], T.er[:, t * S + o:t * S + o + H],
+                                           IDENT, bias=-256.0), "a_e%d" % k)
+
+    def own_u(t, toks, bias):
+        wait("A", *toks)
+        a = 2 * (t - 1)
+        return sig(A.activation(T.hu[:, a:a + 2, :], T.Tt[:, a:a + 2, 0:C], IDENT, bias=bias), "a_hu")
+
+    wait("P", v_ls, d_e[0])
+    p_h = [sig(sums(k, T.Ls, T.er, H * k, 0, Q, True, True), "p_h%d" % k) for k in range(2)]
+    wait("P", v_c128)
+    for par in range(2):
+        ins = P.matmul(T.RC[:, par, 0:16], T.Ls[:, par, 5:133], T.c128[:], True, True)
+    p_c = sig(ins, "p_c")
+    v_t = [turn(0, k, p_h[k]) for k in range(2)]
+    wait("V", p_c)
+    v_tc = sig(V.transpose(T.Tc[:], T.RC[:, :, 0:16]), "v_tc")
+    wo, ws = w_ops(0, 0, 2, v_t)
+    if first:
+        uo, us = u_ops(1, 0, 2, v_t)
+    for i in range(3):
+        wo[i]()
+        if first:
+            uo[i]()
+    wait("V", ws["c"], d_t[0])
+    for i in range(NP):
+        scatter(0, 0, T.er, 0, i)
+    wait("V", d_t[1])
+    v_s = scatter(0, 1, T.er, 0)
+    if not last:
+        wait("g", v_tc)
+        send(T.cvin[:, 0:1], T.Tc[:, Q:Q + 1], "r_c", "l_c")
+    shift_e(1)
+    if not first:
+        r_c = owe("r_c", ieng)
+        a_hu = own_u(1, v_t + [r_c], T.cvin[:, 0:1])
+        wait("A", v_tc)
+        a_b2 = sig(A.activation(T.bias2[:, 0:1], T.Tc[:, 0:1], IDENT, bias=T.cvin[:, 0:1]), "a_b2")
+        shift_e(2)
+    wait("P", v_lg, g_id)
+
+    for t in range(1, M):
+        final = t == M - 1
+        tail = final and last
+        base = (t - 1) * S
+        vg, sgn, p_h, p_x, a_x, v_t = {}, {}, {}, {}, {}, {}
+
+        def piece(k, h):
+            cut = TW if tail and k == 1 else PA
+            return ((0, cut) if h == 0 else (cut, Q)) + (h == 1 and k == 1,)
+
+        def offsets(k):
+            if first:
+                wait("V", us["c"])
+                return
+            uo, st = u_ops(t, k, k + 1, [a_hu, owe("r_b%d" % (2 * (t - 1) + k), ieng)])
+            for f in uo:
+                f()
+            wait("V", st["c"])
+
+        def gather(k, h):
+            qa, qb, _ = piece(k, h)
+            a, b = base + H * k + 64 * qa, base + H * k + 64 * qb
+            wait("V", v_s, d_t[2], a_e[(t, k)])
+            vg[(k, h)] = sig(V.tensor_tensor(T.sp[:, a:b], T.tb[:, 0:W].indirect(T.offu[:, 2 * (t - 1) + k, 4 * qa:4 * qb]),
+                                             T.ep[:, a:b], add), "v_g%d%d" % (k, h))
+
+        def finish(k, h):
+            qa, qb, byv = piece(k, h)
+            a, b = base + H * k + 64 * qa, base + H * k + 64 * qb
+            if byv:
+                wait("V", vg[(k, h)])
+                ins = V.tensor_scalar(T.sg[:, a:b], T.sp[:, a:b], 0.0, 0.5, AluOpType.is_ge, sub)
+            else:
+                wait("A", vg[(k, h)])
+                ins = A.activation(T.sg[:, a:b], T.sp[:, a:b], SIGN, bias=0.5)
+            sgn[(k, h)] = sig(ins, "a_s%d%d" % (k, h))
+            if tail:
+                return
+            wait("P", vg[(k, h)])
+            sums(k, T.Ls, T.sp, base + H * k, qa, qb, h == 0, False)
+            wait("P", sgn[(k, h)])
+            ins = sums(k, T.Lh if byv else T.Lg, T.sg, base + H * k, qa, qb, False, h == 1)
+            if h == 1:
+                p_h[k] = sig(ins, "p_h%d" % k)
+
+        def x_mm(k, hs):
+            o = base + H * k
+            w = 64 * piece(k, hs[-1])[1]
+            wait("P", *[sgn[(k, h)] for h in hs])
+            P.matmul(X[k][:, 0:w], T.idp[:], T.sp[:, o:o + w], True, False)
+            if piece(k, hs[-1])[2]:
+                c = 64 * PA
+                P.matmul(X[k][:, 0:c], T.idn[:], T.sg[:, o:o + c], False, False)
+                ins = P.matmul(X[k][:, c:w], T.idh[:], T.sg[:, o + c:o + w], False, True)
+            else:
+                ins = P.matmul(X[k][:, 0:w], T.idn[:], T.sg[:, o:o + w], False, True)
+            p_x[k] = (sig(ins, "p_x%d" % k), w)
+
+        def x_out(k):
+            o = base + H * k
+            tok, w = p_x[k]
+            wait("A", tok)
+            a_x[k] = sig(A.activation(T.xs[:, o:o + w], X[k][:, 0:w], IDENT, bias=128.0), "a_x%d" % k)
+
+        def pass_on(k):
+            v_t[k] = turn(t, k, p_h[k])
+            if last:
+                return None
+            wait("g", v_t[k])
+            i = 2 * (t - 1) + k
+            return send(T.land[:, i, :], T.Tt[:, 2 * t + k, C:2 * C], "r_b%d" % i, "l_%d" % t)
+
+        offsets(0)
+        gather(0, 0)
+        finish(0, 0)
+        gather(0, 1)
+        finish(0, 1)
+        if tail or not final:
+            x_mm(0, (0, 1))
+        if tail:
+            x_out(0)
+        offsets(1)
+        gather(1, 0)
+        finish(1, 0)
+        if tail:
+            x_mm(1, (0,))
+            gather(1, 1)
+            x_out(1)
+            a, b = base + H + 64 * TW, base + S
+            wait("V", vg[(1, 1)])
+            v_m = sig(V.tensor_scalar(T.mm[:, 0:b - a], T.sp[:, a:b], 0.0, 256.0, AluOpType.is_lt, mul), "v_m")
+            wait("V", v_m)
+            v_x = sig(V.tensor_tensor(T.xs[:, a:b], T.sp[:, a:b], T.mm[:, 0:b - a], add), "v_x")
+            wait("D", a_x[0])
+            store(t * S, t * S + H)
+            wait("D", a_x[1], v_x)
+            store(t * S + H, (t + 1) * S)
+            break
+        pass_on(0)
+        gather(1, 1)
+        if final:
+            finish(1, 1)
+            for k in range(2):
+                x_mm(k, (0, 1))
+                x_out(k)
+            left = pass_on(1)
+        else:
+            x_out(0)
+            wo, ws0 = w_ops(t, 0, 1, [v_t[0]])
+            wo[0]()
+            finish(1, 1)
+            x_mm(1, (0, 1))
+            x_out(1)
+            wo[1]()
+            wo[2]()
+            left = pass_on(1)
+            wo, ws1 = w_ops(t, 1, 2, [v_t[1]])
+            if first:
+                uo, us = u_ops(t + 1, 0, 2, [v_t[0], v_t[1], v_tc])
+            wait("V", ws0["c"], a_x[0], *vg.values())
+            for i in range(NP):
+                scatter(t, 0, T.xs, base, i)
+                if i < 3:
+                    wo[i]()
+                    if first:
+                        uo[i]()
+            wait("V", ws1["c"], a_x[1])
+            v_s = scatter(t, 1, T.xs, base)
+            if not first:
+                a_hu = own_u(t + 1, [v_t[0], v_t[1], a_b2], T.bias2[:, 0:1])
+        wait("D", left)
+        if first and t + 2 < M:
+            load_e(t + 2, t + 3)
+        if first and not final:
+            shift_e(t + 1)
+        if not first and t + 2 < M:
+            shift_e(t + 2)
+        if rank >= n - 2:
+            wait("D", a_x[0], a_x[1])
+            store(t * S, (t + 1) * S)
+        elif final:
+            wait("D", a_x[0], a_x[1])
+            store(S, M * S)
+            if first:
+                store0()
+
+    for name in cnt:
+        if done.get(name, 0) < cnt[name]:
+            wait("g" if name[0] == "l" else "D", (name, cnt[name]))

@@ -4,9 +4,23 @@ W, S, M = 8192, 768, 5
 H = S // 2
 C = H // 16
 Q = 6
-PA = 3
-TW = 2
-NP = 4
+BIG = float(2 ** 20)
+MAGIC = 1.5 * 2 ** 26
+
+GP = {"first": ((2, 2, 2), (4, 2)), "next": ((2, 2, 2), (4, 2)), "final": ((2, 2, 2), (4, 2)),
+      "tail": ((2, 2, 2), (2, 2, 2))}
+SP = ((2, 2, 2), (3, 3))
+FUSE = (True, False)
+V_ZERO = "T0 w00 T1 Tc w01 w10 n1 S00 w11 S01 S02 S10 n2 S11 S12"
+V_ZERO_NEXT = "T0 T1 w00 Tc w10 w01 w11 S00 S01 S02 S10 S11 S12 d n0 n1 n2"
+V_FIRST = "G00 G01 G02 G10 G11 G12 m0 T0 w00 w01 m1 T1 S00 w10 S01 n1 w11 S02 n2 S10 S11 S12"
+V_NEXT = "G00 u0 u1 G01 u2 G02 G10 G11 G12 T0 w00 m0 w01 m1 T1 S00 w10 S01 d w11 S02 S10 n0 n1 S11 n2 S12"
+V_FINAL = "G00 u0 u1 G01 u2 G02 G10 G11 G12 T0 T1"
+V_TAIL = "G00 u0 u1 G01 u2 G02 G10 G11 G12 m1 x11 x12"
+A_STEP = "s00 s01 s02 s10 s11 s12 e n0 r x1 h x0"
+A_TAIL = "s00 s01 s02 s10 s11 x0 x10 x11"
+P_STEP = "a00 a01 b00 a02 b01 b02 a10 a11 b10 a12 b11 b12 X1 X0 k0 k1"
+P_TAIL = "X0 X10 X11"
 
 SCRATCH = {
     "tb": ("sbuf", [128, W], "bfloat16"),
@@ -15,36 +29,32 @@ SCRATCH = {
     "sp": ("sbuf", [128, 4 * S], "bfloat16"),
     "sg": ("sbuf", [128, 4 * S], "bfloat16"),
     "xs": ("sbuf", [128, 4 * S], "bfloat16"),
-    "mm": ("sbuf", [128, H], "bfloat16"),
+    "mm": ("sbuf", [128, S], "bfloat16"),
     "hws": ("sbuf", [128, 16], "bfloat16"),
     "Ls": ("sbuf", [128, 2, 160], "bfloat16"),
     "Lg": ("sbuf", [128, 2, 160], "bfloat16"),
-    "Lh": ("sbuf", [128, 2, 160], "bfloat16"),
     "Gp": ("sbuf", [128, 2, 4], "bfloat16"),
     "one8": ("sbuf", [128, 2, 4], "bfloat16"),
     "ones": ("sbuf", [128, 128], "bfloat16"),
     "negs": ("sbuf", [128, 128], "bfloat16"),
-    "negh": ("sbuf", [128, 128], "bfloat16"),
     "idp": ("sbuf", [128, 128], "bfloat16"),
     "idn": ("sbuf", [128, 128], "bfloat16"),
-    "idh": ("sbuf", [128, 128], "bfloat16"),
     "c128": ("sbuf", [128, 16], "bfloat16"),
-    "pint": ("sbuf", [128, 8], "int32"),
-    "mint": ("sbuf", [128, 8], "int32"),
-    "mflt": ("sbuf", [128, 8], "float32"),
-    "c16": ("sbuf", [128, 2, C], "float32"),
-    "jj": ("sbuf", [128, 2, C], "float32"),
+    "Kc": ("sbuf", [128, 2, 4, 32], "bfloat16"),
+    "Kr": ("sbuf", [128, 64], "bfloat16"),
     "Tt": ("sbuf", [128, 2 * M, 128], "float32"),
     "Tc": ("sbuf", [128, 32], "float32"),
     "cvin": ("sbuf", [128, 8], "float32"),
-    "bias2": ("sbuf", [128, 8], "float32"),
+    "col": ("sbuf", [128, 8], "float32"),
     "land": ("sbuf", [128, 8, C], "float32"),
-    "hu": ("sbuf", [128, 8, C], "float32"),
-    "hi": ("sbuf", [128, 8, C], "int32"),
-    "hj": ("sbuf", [128, 8, C], "int32"),
+    "ru": ("sbuf", [128, 8, C], "bfloat16"),
+    "du": ("sbuf", [128, 8, C], "float32"),
+    "h1": ("sbuf", [128, 8, C], "float32"),
+    "h2": ("sbuf", [128, 8, C], "float32"),
+    "hr": ("sbuf", [128, 8, C], "bfloat16"),
+    "ha": ("sbuf", [128, 8, C], "float32"),
     "offu": ("sbuf", [128, 8, C], "uint16"),
-    "qw": ("sbuf", [128, 8, C], "int32"),
-    "fw": ("sbuf", [128, 8, C], "float32"),
+    "rw": ("sbuf", [128, 8, C], "float32"),
     "offw": ("sbuf", [128, 8, C], "uint16"),
     "R0": ("psum", [128, 2, 512], "float32"),
     "R1": ("psum", [128, 2, 512], "float32"),
@@ -53,15 +63,13 @@ SCRATCH = {
     "X1": ("psum", [128, 512], "float32"),
 }
 SEMAPHORES = (
-    ["d_hw", "d_e0", "d_e1", "d_e2", "d_e3", "d_e4", "d_t0", "d_t1", "d_t2", "d_y"]
-    + ["v_one8", "v_z", "v_ones", "v_c128", "v_m0", "v_m1", "v_jj", "v_ls", "v_lg", "v_tc"]
-    + ["g_g0", "g_g1", "g_pi", "g_c16", "g_id"]
-    + ["p_c", "p_h0", "p_h1", "p_x0", "p_x1"]
-    + ["a_b2", "a_hu", "a_e0", "a_e1", "a_s00", "a_s01", "a_s10", "a_s11", "a_x0", "a_x1"]
-    + ["v_g00", "v_g01", "v_g10", "v_g11", "v_t0", "v_t1", "v_ua", "v_ub", "v_uc", "v_wa", "v_wb", "v_wc",
-       "v_s", "v_m", "v_x"]
+    ["V", "A", "P", "g", "d_hw", "d_e0", "d_e1", "d_e2", "d_e3", "d_e4", "d_t0", "d_t1", "d_t2", "d_y"]
     + ["r_c", "l_c"] + ["r_b%d" % i for i in range(8)] + ["l_%d" % t for t in range(1, M)]
 )
+
+
+def cuts(parts):
+    return [(sum(parts[:i]), sum(parts[:i + 1])) for i in range(len(parts))]
 
 
 def rank_program(g, core, T, topo):
@@ -71,6 +79,7 @@ def rank_program(g, core, T, topo):
     n = len(T.cores)
     first, last = rank == 0, rank == n - 1
     V, A, P, D = g.vector, g.scalar, g.tensor, g.sync
+    queue = {"V": V, "A": A, "P": P, "D": D, "g": g}
     add, sub, mul = AluOpType.add, AluOpType.subtract, AluOpType.mult
     IDENT, SIGN = ActivationFunctionType.Identity, ActivationFunctionType.Sign
     cnt, seen, done = {}, {}, {}
@@ -84,13 +93,30 @@ def rank_program(g, core, T, topo):
         return (name, cnt[name])
 
     def wait(qn, *toks):
-        q = {"V": V, "A": A, "P": P, "D": D, "g": g}[qn]
-        for tok in toks:
-            if tok is None or seen.get((qn, tok[0]), 0) >= tok[1]:
-                continue
-            q.wait_ge(T.sem[tok[0]], tok[1])
-            seen[(qn, tok[0])] = tok[1]
-            done[tok[0]] = max(done.get(tok[0], 0), tok[1])
+        most = {}
+        for name, k in toks:
+            most[name] = max(most.get(name, 0), k)
+        for name, k in most.items():
+            if seen.get((qn, name), 0) < k:
+                queue[qn].wait_ge(T.sem[name], k)
+                seen[(qn, name)] = k
+                done[name] = max(done.get(name, 0), k)
+
+    tok = {}
+
+    def emit(orders, calls):
+        todo = {q: [c for c in order if c in calls and calls[c][0] == q] for q, order in orders.items()}
+        assert sum(len(v) for v in todo.values()) == len(calls)
+        while any(todo.values()):
+            moved = False
+            for q, names in todo.items():
+                while names and all(d in tok for d in calls[names[0]][1]):
+                    name = names.pop(0)
+                    wait(q, *[tok[d] for d in calls[name][1]])
+                    ins = calls[name][2]()
+                    tok[name] = ins if isinstance(ins, tuple) else sig(ins, q)
+                    moved = True
+            assert moved, todo
 
     if not last:
         nxt = T.cores[rank + 1]
@@ -98,71 +124,84 @@ def rank_program(g, core, T, topo):
         omask, oeng = topo.mask(core, nxt), len(topo.engines(core, nxt))
     if not first:
         ieng = len(topo.engines(T.cores[rank - 1], core))
+        tok["cv"] = owe("r_c", ieng)
+        for i in range(8):
+            tok["land", i] = owe("r_b%d" % i, ieng)
 
     def send(dst, src, rsem, lsem):
         g.remote_dma(dst, src, T.sem[rsem], T.sem[lsem], pid, rid, omask)
         return owe(lsem, oeng)
 
     d_hw = sig(A.dma_start(T.hws[:, 0:3], T.hw[:]), "d_hw", 16)
-    d_e = {}
 
     def load_e(t0, t1):
-        tok = sig(D.dma_start(T.er[:, t0 * S:t1 * S], T.res[:, t0 * S:t1 * S]), "d_e%d" % t0, 16)
+        d = sig(D.dma_start(T.er[:, t0 * S:t1 * S], T.res[:, t0 * S:t1 * S]), "d_e%d" % t0, 16)
         for t in range(t0, t1):
-            d_e[t] = tok
+            tok["er", t] = d
+        return d
 
     def load_t(i, a, b):
-        return sig(D.dma_start(T.tb[:, a:b], T.tab[:, a:b]), "d_t%d" % i, 16)
+        tok["tb", i] = sig(D.dma_start(T.tb[:, a:b], T.tab[:, a:b]), "d_t%d" % i, 16)
 
     load_e(0, 1)
-    d_t = [load_t(0, 0, 8 * H), load_t(1, 8 * H, 8 * S)]
+    load_t(0, 0, 8 * H)
+    load_t(1, 8 * H, 8 * S)
     load_e(1, 2)
-    d_t.append(load_t(2, 8 * S, W))
+    load_t(2, 8 * S, W)
     load_e(2, 3 if first else M)
 
     def store(a, b):
-        sig(D.dma_start(T.y[:, a:b], T.xs[:, a - S:b - S]), "d_y", 16)
+        return sig(D.dma_start(T.y[:, a:b], T.xs[:, a - S:b - S]), "d_y", 16)
 
     def store0():
-        wait("D", d_e[0])
-        sig(D.dma_start(T.y[:, 0:S], T.er[:, 0:S]), "d_y", 16)
+        wait("D", tok["er", 0])
+        return sig(D.dma_start(T.y[:, 0:S], T.er[:, 0:S]), "d_y", 16)
 
     if not first:
         store0()
 
-    v_one8 = sig(V.memset(T.one8[:], 1.0), "v_one8")
-    for L in (T.Ls, T.Lg, T.Lh):
-        v_z = sig(V.memset(L[:], 0.0), "v_z")
-    for b, c in ((T.ones, 1.0), (T.negs, -128.0), (T.negh, -256.0)):
-        v_ones = sig(V.memset(b[:], c), "v_ones")
-    v_c128 = sig(V.memset(T.c128[:], 128.0), "v_c128")
-    g_pi = sig(g.iota(T.pint[:, 0:1], [[0, 1]], 0, 1), "g_pi")
-    wait("g", v_one8)
-    g0 = sig(g.affine_select(T.Gp[:], T.one8[:], [[-16, 2], [-32, 4]], AluOpType.is_ge, 0.0, 0, 1), "g_g0")
-    sig(g.iota(T.c16[:, 0, :], [[0, NP], [16, C // NP]], 0, 0, allow_small_or_imprecise_dtypes=True), "g_c16")
-    g_c16 = sig(g.iota(T.c16[:, 1, :], [[16, C]], 0, 0, allow_small_or_imprecise_dtypes=True), "g_c16")
+    def iota(out, pattern):
+        return g.iota(out, pattern, 0, 0, allow_small_or_imprecise_dtypes=True)
+
+    v_one8 = sig(V.memset(T.one8[:], 1.0), "V")
+    v_kc = sig(V.memset(T.Kc[0:64], 0.0), "V")
+    wait("g", v_one8, sig(iota(T.Kr[32:64, :], [[8, 64]]), "g"))
+    g0 = sig(g.affine_select(T.Gp[:], T.one8[:], [[-16, 2], [-32, 4]], AluOpType.is_ge, 0.0, 0, 1), "g")
+    wait("g", v_kc)
+    for k in range(2):
+        if len(set(SP[k])) == 1:
+            iota(T.Kc[0:1, k, :, 3 * Q:4 * Q], [[0, 4], [0, len(SP[k])], [512, SP[k][0]]])
+        else:
+            for a, b in cuts(SP[k]):
+                iota(T.Kc[0:1, k, :, 3 * Q + a:3 * Q + b], [[0, 4], [512, b - a]])
     wait("g", g0)
-    g1 = sig(g.affine_select(T.Gp[:], T.Gp[:], [[16, 2], [32, 4]], AluOpType.is_ge, 0.0, 15, -1), "g_g1")
+    g1 = sig(g.affine_select(T.Gp[:], T.Gp[:], [[16, 2], [32, 4]], AluOpType.is_ge, 0.0, 15, -1), "g")
+    V.memset(T.Ls[:], 0.0)
+    V.memset(T.Lg[:], 0.0)
+    V.memset(T.ones[:], 1.0)
+    v_ones = sig(V.memset(T.negs[:], -128.0), "V")
+    wait("V", v_kc)
+    V.memset(T.Kc[0:1, :, :, 2 * Q:3 * Q], -3.5)
+    V.memset(T.Kc[32:33, :, :, 3 * Q:4 * Q], 1.0)
+    V.memset(T.Kr[0:32, :], 1.0)
+    v_z = sig(V.memset(T.c128[:], 128.0), "V")
     wait("g", v_ones)
-    for o, b in ((T.idp, T.ones), (T.idn, T.negs), (T.idh, T.negh)):
-        g_id = sig(g.affine_select(o[:], b[:], [[-1, 128]], AluOpType.is_equal, 0.0, 0, 1), "g_id")
-    wait("V", g_pi)
-    m0 = sig(V.tensor_scalar(T.mint[:, 0:1], T.pint[:, 0:1], 15, None, AluOpType.bitwise_and), "v_m0")
-    wait("V", m0)
-    m1 = sig(V.tensor_copy(T.mflt[:, 0:1], T.mint[:, 0:1]), "v_m1")
-    wait("V", m1, g_c16)
-    v_jj = sig(V.tensor_scalar(T.jj[:], T.c16[:], T.mflt[:, 0:1], 0.4375, add, add), "v_jj")
+    for o, b in ((T.idp, T.ones), (T.idn, T.negs)):
+        tok["id"] = sig(g.affine_select(o[:], b[:], [[-1, 128]], AluOpType.is_equal, 0.0, 0, 1), "g")
     wait("V", v_z, g1, d_hw)
-    for kind, scale in ((2, 0.125), (0, 1.0), (1, 1.0)):
-        o = 5 + Q * kind
-        v_ls = sig(V.tensor_scalar(T.Ls[:, :, o:o + 128:32], T.Gp[:], T.hws[:, kind:kind + 1], scale, mul, mul), "v_ls")
-    for L, scale in ((T.Lg, -128.0), (T.Lh, -256.0)):
-        for kind in (0, 1):
-            o = 5 + Q * kind
-            v_lg = sig(V.tensor_scalar(L[:, :, o:o + 128:32], T.Gp[:], T.hws[:, kind:kind + 1], scale, mul, mul), "v_lg")
+    for L, kinds, scale in ((T.Ls, (2, 3, 0, 1), 1.0), (T.Lg, (0, 1), -128.0)):
+        for kind in kinds:
+            o, w = 5 + Q * kind, min(kind, 2)
+            ins = V.tensor_scalar(L[:, :, o:o + 128:32], T.Gp[:], T.hws[:, w:w + 1], scale, mul, mul)
+        tok[L.name] = sig(ins, "V")
 
     R = [T.R0, T.R1]
     X = [T.X0, T.X1]
+
+    def opening(k):
+        for par in range(2):
+            ins = P.matmul(R[k][:, par, 0:64], T.Kc[0:64, k], T.Kr[0:64, :], True, False)
+        return ins
 
     def sums(k, L, src, base, q0, q1, start, stop):
         ins = None
@@ -172,250 +211,200 @@ def rank_program(g, core, T, topo):
                                start and q == q0, stop and q == q1 - 1)
         return ins
 
-    def turn(t, k, tok):
-        wait("V", tok)
+    def turn(t, k):
         for b in range(4):
-            out = sig(V.transpose(T.Tt[:, 2 * t + k, b:128:4], R[k][:, :, 16 * b:16 * b + 16]), "v_t%d" % k)
-        return out
+            ins = V.transpose(T.Tt[:, 2 * t + k, b:128:4], R[k][:, :, 16 * b:16 * b + 16])
+        return ins
 
-    def w_ops(t, k0, k1, tok):
-        a, b = 2 * t + k0, 2 * t + k1
-        st = {}
+    def w_calls(t, k):
+        i = 2 * t + k
+        return {
+            (t, "w%d0" % k): ("V", [(t, "T%d" % k)], lambda: V.tensor_scalar(
+                T.rw[:, i, :], T.Tt[:, i, 2 * C:3 * C], MAGIC, MAGIC, add, sub)),
+            (t, "w%d1" % k): ("V", [(t, "w%d0" % k)], lambda: V.tensor_tensor(
+                T.offw[:, i, :], T.Tt[:, i, 3 * C:4 * C], T.rw[:, i, :], sub)),
+        }
 
-        def wa():
-            wait("V", v_jj, *tok)
-            st["a"] = sig(V.tensor_tensor(T.qw[:, a:b, :], T.Tt[:, a:b, 2 * C:3 * C], T.jj[:, k0:k1, :], sub), "v_wa")
-
-        def wb():
-            wait("V", st["a"])
-            st["b"] = sig(V.tensor_tensor(T.fw[:, a:b, :], T.Tt[:, a:b, 2 * C:3 * C], T.qw[:, a:b, :], sub), "v_wb")
-
-        def wc():
-            wait("V", st["b"])
-            st["c"] = sig(V.tensor_scalar(T.offw[:, a:b, :], T.fw[:, a:b, :], 8.0, None, mul), "v_wc")
-        return [wa, wb, wc], st
-
-    def u_ops(t, k0, k1, tok):
+    def u_calls(t, k0, k1, name):
         a, b = 2 * (t - 1) + k0, 2 * (t - 1) + k1
-        st = {}
+        s, c = name
+        if first:
+            deps = [(t - 1, "T0"), (t - 1, "T1"), "col"]
+            lo, hi = (BIG + W - 4095.5, BIG + W) if t == 1 else (T.col[:, 0:1], T.col[:, 1:2])
+            calls = {(s, c + "0"): ("A", deps, lambda: A.activation(T.hr[:, a:b, :], T.Tt[:, a:b, 0:C], IDENT, bias=lo)),
+                     (s, c + "1"): ("V", deps, lambda: V.tensor_scalar(T.ha[:, a:b, :], T.Tt[:, a:b, 0:C], hi, None, add))}
+        else:
+            deps = [(t - 1, "h"), ("land", a)]
+            calls = {(s, c + "0"): ("V", deps, lambda: V.tensor_tensor(T.hr[:, a:b, :], T.h1[:, a:b, :], T.land[:, a:b, :], add)),
+                     (s, c + "1"): ("V", deps, lambda: V.tensor_tensor(T.ha[:, a:b, :], T.h2[:, a:b, :], T.land[:, a:b, :], add))}
+        calls[s, c + "2"] = ("V", [(s, c + "0"), (s, c + "1")], lambda: V.tensor_tensor(
+            T.offu[:, a:b, :], T.ha[:, a:b, :], T.hr[:, a:b, :], sub))
+        return calls
 
-        def ua():
-            wait("V", *tok)
-            if not first:
-                ins = V.tensor_tensor(T.hi[:, a:b, :], T.hu[:, a:b, :], T.land[:, a:b, :], add)
-            elif t == 1:
-                ins = V.tensor_copy(T.hi[:, a:b, :], T.Tt[:, a:b, 0:C])
-            else:
-                ins = V.tensor_scalar(T.hi[:, a:b, :], T.Tt[:, a:b, 0:C], T.Tc[:, 0:1], None, add)
-            st["a"] = sig(ins, "v_ua")
+    def s_calls(t, src, base, deps):
+        calls = {}
+        for k in range(2):
+            for i, (a, b) in enumerate(cuts(SP[k])):
+                def scatter(k=k, a=a, b=b):
+                    win = T.tb[:, 8 * H * k + 512 * a:8 * H * k + 512 * b].indirect(T.offw[:, 2 * t + k, 4 * a:4 * b])
+                    o = base + H * k
+                    if t and FUSE[k]:
+                        return V.tensor_tensor(win, T.sp[:, o + 64 * a:o + 64 * b],
+                                               T.mm[:, H * k + 64 * a:H * k + 64 * b], add)
+                    return V.tensor_copy(win, src[:, o + 64 * a:o + 64 * b])
+                calls[t, "S%d%d" % (k, i)] = ("V", [(t, "w%d1" % k)] + deps(k), scatter)
+        return calls
 
-        def ub():
-            wait("V", st["a"])
-            st["b"] = sig(V.tensor_scalar(T.hj[:, a:b, :], T.hi[:, a:b, :], W - 1, None, AluOpType.bitwise_and), "v_ub")
+    def x_mm(bank, a, b):
+        P.matmul(bank, T.idp[:], T.sp[:, a:b], True, False)
+        return P.matmul(bank, T.idn[:], T.sg[:, a:b], False, True)
 
-        def uc():
-            wait("V", st["b"])
-            st["c"] = sig(V.tensor_copy(T.offu[:, a:b, :], T.hj[:, a:b, :]), "v_uc")
-        return [ua, ub, uc], st
+    def x_out(bank, a, b):
+        return A.activation(T.xs[:, a:b], bank, IDENT, bias=128.0)
 
-    def scatter(t, k, src, base, i=0):
-        a, b = (0, C) if k else (i * C // NP, (i + 1) * C // NP)
-        win = T.tb[:, 8 * H * k + 128 * a:8 * H * k + 128 * b]
-        o = base + H * k
-        return sig(V.tensor_copy(win.indirect(T.offw[:, 2 * t + k, a:b]), src[:, o + 16 * a:o + 16 * b]), "v_s")
-
-    a_e = {}
+    def wrap(o, a, b):
+        return V.tensor_scalar(T.mm[:, o:o + b - a], T.sp[:, a:b], 0.0, 256.0, AluOpType.is_lt, mul)
 
     def shift_e(t):
-        wait("A", d_e[t])
-        for k in range(2):
-            o = H * k
-            a_e[(t, k)] = sig(A.activation(T.ep[:, (t - 1) * S + o:(t - 1) * S + o + H], T.er[:, t * S + o:t * S + o + H],
-                                           IDENT, bias=-256.0), "a_e%d" % k)
+        return A.activation(T.ep[:, (t - 1) * S:t * S], T.er[:, t * S:(t + 1) * S], IDENT, bias=-256.0)
 
-    def own_u(t, toks, bias):
-        wait("A", *toks)
-        a = 2 * (t - 1)
-        return sig(A.activation(T.hu[:, a:a + 2, :], T.Tt[:, a:a + 2, 0:C], IDENT, bias=bias), "a_hu")
+    def h_calls(t):
+        a, b = 2 * t, 2 * t + 2
+        u = T.Tt[:, a:b, 0:C]
+        up, lo, hi = ((T.col[:, 0:1], T.col[:, 3:4], T.col[:, 4:5]) if t else (BIG + 0.5, T.col[:, 1:2], T.col[:, 2:3]))
 
-    wait("P", v_ls, d_e[0])
-    p_h = [sig(sums(k, T.Ls, T.er, H * k, 0, Q, True, True), "p_h%d" % k) for k in range(2)]
-    wait("P", v_c128)
-    for par in range(2):
-        ins = P.matmul(T.RC[:, par, 0:16], T.Ls[:, par, 5:133], T.c128[:], True, True)
-    p_c = sig(ins, "p_c")
-    v_t = [turn(0, k, p_h[k]) for k in range(2)]
-    wait("V", p_c)
-    v_tc = sig(V.transpose(T.Tc[:], T.RC[:, :, 0:16]), "v_tc")
-    wo, ws = w_ops(0, 0, 2, v_t)
-    if first:
-        uo, us = u_ops(1, 0, 2, v_t)
-    for i in range(3):
-        wo[i]()
-        if first:
-            uo[i]()
-    wait("V", ws["c"], d_t[0])
-    for i in range(NP):
-        scatter(0, 0, T.er, 0, i)
-    wait("V", d_t[1])
-    v_s = scatter(0, 1, T.er, 0)
+        def both():
+            A.activation(T.h1[:, a:b, :], T.du[:, a:b, :], IDENT, bias=lo)
+            return A.activation(T.h2[:, a:b, :], T.du[:, a:b, :], IDENT, bias=hi)
+
+        return {(t, "r"): ("A", [(t, "T0"), (t, "T1"), "col"], lambda: A.activation(T.ru[:, a:b, :], u, IDENT, bias=up)),
+                (t, "d"): ("V", [(t, "r")], lambda: V.tensor_tensor(T.du[:, a:b, :], u, T.ru[:, a:b, :], sub)),
+                (t, "h"): ("A", [(t, "d"), "col2"], both)}
+
+    def named(t, order):
+        return [c if c in ("Tc", "pc", "cs", "col", "col1", "col2") else (t, c) for c in order.split()]
+
+    calls = {(0, "e"): ("A", [("er", 1)], lambda: shift_e(1))}
+    wait("P", v_z, g1)
+    for k in range(2):
+        opening(k)
+        calls[0, "b%d" % k] = ("P", ["Ls", ("er", 0)], lambda k=k: sums(k, T.Ls, T.er, H * k, 0, Q, False, True))
+        calls[0, "T%d" % k] = ("V", [(0, "b%d" % k)], lambda k=k: turn(0, k))
+        calls[0, "k%d" % k] = ("P", [(0, "T%d" % k)], lambda k=k: opening(k))
+        calls.update(w_calls(0, k))
+
+    def const_sums():
+        for par in range(2):
+            ins = P.matmul(T.RC[:, par, 0:16], T.Ls[:, par, 5:133], T.c128[:], True, True)
+        return ins
+
+    def column(i, src, bias):
+        return A.activation(T.col[:, i:i + 1], src, IDENT, bias=bias)
+
+    cu, cv = T.Tc[:, 0:1], T.cvin[:, 0:1]
+    calls["pc"] = ("P", [], const_sums)
+    calls["Tc"] = ("V", ["pc"], lambda: V.transpose(T.Tc[:], T.RC[:, :, 0:16]))
+    calls.update(s_calls(0, T.er, 0, lambda k: [("tb", k)]))
     if not last:
-        wait("g", v_tc)
-        send(T.cvin[:, 0:1], T.Tc[:, Q:Q + 1], "r_c", "l_c")
-    shift_e(1)
-    if not first:
-        r_c = owe("r_c", ieng)
-        a_hu = own_u(1, v_t + [r_c], T.cvin[:, 0:1])
-        wait("A", v_tc)
-        a_b2 = sig(A.activation(T.bias2[:, 0:1], T.Tc[:, 0:1], IDENT, bias=T.cvin[:, 0:1]), "a_b2")
-        shift_e(2)
-    wait("P", v_lg, g_id)
+        calls["cs"] = ("g", ["Tc"], lambda: send(T.cvin[:, 0:1], T.Tc[:, Q:Q + 1], "r_c", "l_c"))
+    if first:
+        tok["col"] = tok["Ls"]
+        calls.update(u_calls(1, 0, 2, (0, "n")))
+        calls["col1"] = ("A", ["Tc"], lambda: [column(0, cu, BIG + W - 4095.5), column(1, cu, BIG + W)][1])
+    else:
+        calls.update(u_calls(1, 0, 1, (0, "n")))
+        calls.update(h_calls(0))
+        calls["col"] = ("A", ["Tc"], lambda: column(0, cu, BIG + 0.5))
+        calls["col1"] = ("A", ["cv"], lambda: [column(1, cv, 2 * BIG + W - 4095.5), column(2, cv, 2 * BIG + W)][1])
+        calls["col2"] = ("A", ["col1"], lambda: [column(3, cu, T.col[:, 1:2]), column(4, cu, T.col[:, 2:3])][1])
+    emit({"P": named(0, "b0 b1 pc k0 k1"), "V": named(0, V_ZERO if first else V_ZERO_NEXT), "g": ["cs"],
+          "A": named(0, "n0 col r e col1 col2 h")}, calls)
+    if first:
+        tok["col"] = tok["col1"]
+    wait("P", tok["Lg"], tok["id"])
 
     for t in range(1, M):
         final = t == M - 1
         tail = final and last
         base = (t - 1) * S
-        vg, sgn, p_h, p_x, a_x, v_t = {}, {}, {}, {}, {}, {}
+        calls = {}
+        table = [(t - 1, "S%d%d" % (k, i)) for k in range(2) for i in range(len(SP[k]))] + [("tb", 2), (t - 1, "e")]
+        gp = GP["tail" if tail else "final" if final else "first" if first else "next"]
+        every = lambda c, ks: [(t, "%s%d%d" % (c, k, h)) for k in ks for h in range(len(gp[k]))]
+        issued = {0: [], 1: []}
 
-        def piece(k, h):
-            cut = TW if tail and k == 1 else PA
-            return ((0, cut) if h == 0 else (cut, Q)) + (h == 1 and k == 1,)
+        def part(k, L, src, qa, qb):
+            issued[k].append(qa)
+            return sums(k, L, src, base + H * k, qa, qb, final and len(issued[k]) == 1, len(issued[k]) == 2 * len(gp[k]))
 
-        def offsets(k):
-            if first:
-                wait("V", us["c"])
-                return
-            uo, st = u_ops(t, k, k + 1, [a_hu, owe("r_b%d" % (2 * (t - 1) + k), ieng)])
-            for f in uo:
-                f()
-            wait("V", st["c"])
+        for k in range(2):
+            for h, (qa, qb) in enumerate(cuts(gp[k])):
+                a, b = base + H * k + 64 * qa, base + H * k + 64 * qb
+                kh = "%d%d" % (k, h)
+                off = (t - 1, "n2") if first or k == 0 else (t, "u2")
+                calls[t, "G" + kh] = ("V", table + [off], lambda k=k, qa=qa, qb=qb, a=a, b=b: V.tensor_tensor(
+                    T.sp[:, a:b], T.tb[:, 0:W].indirect(T.offu[:, 2 * (t - 1) + k, 4 * qa:4 * qb]), T.ep[:, a:b], add))
+                calls[t, "s" + kh] = ("A", [(t, "G" + kh)], lambda a=a, b=b: A.activation(
+                    T.sg[:, a:b], T.sp[:, a:b], SIGN, bias=0.5))
+                if not tail:
+                    calls[t, "a" + kh] = ("P", [(t, "G" + kh)], lambda k=k, qa=qa, qb=qb: part(k, T.Ls, T.sp, qa, qb))
+                    calls[t, "b" + kh] = ("P", [(t, "s" + kh)], lambda k=k, qa=qa, qb=qb: part(k, T.Lg, T.sg, qa, qb))
 
-        def gather(k, h):
-            qa, qb, _ = piece(k, h)
-            a, b = base + H * k + 64 * qa, base + H * k + 64 * qb
-            wait("V", v_s, d_t[2], a_e[(t, k)])
-            vg[(k, h)] = sig(V.tensor_tensor(T.sp[:, a:b], T.tb[:, 0:W].indirect(T.offu[:, 2 * (t - 1) + k, 4 * qa:4 * qb]),
-                                             T.ep[:, a:b], add), "v_g%d%d" % (k, h))
-
-        def finish(k, h):
-            qa, qb, byv = piece(k, h)
-            a, b = base + H * k + 64 * qa, base + H * k + 64 * qb
-            if byv:
-                wait("V", vg[(k, h)])
-                ins = V.tensor_scalar(T.sg[:, a:b], T.sp[:, a:b], 0.0, 0.5, AluOpType.is_ge, sub)
+            if tail and k:
+                banks = [T.X1[:, 0:64 * gp[1][0]], T.RC[:, 0, 0:64 * gp[1][1]]]
+                for h, (qa, qb) in enumerate(cuts(gp[1])):
+                    a, b = base + H + 64 * qa, base + H + 64 * qb
+                    if qb < Q:
+                        calls[t, "X1%d" % h] = ("P", [(t, "s1%d" % h)], lambda h=h, a=a, b=b: x_mm(banks[h], a, b))
+                        calls[t, "x1%d" % h] = ("A", [(t, "X1%d" % h)], lambda h=h, a=a, b=b: x_out(banks[h], a, b))
+                    else:
+                        del calls[t, "s1%d" % h]
+                        calls[t, "m1"] = ("V", [(t, "G1%d" % h)], lambda a=a, b=b: wrap(0, a, b))
+                        calls[t, "x1%d" % h] = ("V", [(t, "m1")], lambda a=a, b=b: V.tensor_tensor(
+                            T.xs[:, a:b], T.sp[:, a:b], T.mm[:, 0:b - a], add))
             else:
-                wait("A", vg[(k, h)])
-                ins = A.activation(T.sg[:, a:b], T.sp[:, a:b], SIGN, bias=0.5)
-            sgn[(k, h)] = sig(ins, "a_s%d%d" % (k, h))
-            if tail:
-                return
-            wait("P", vg[(k, h)])
-            sums(k, T.Ls, T.sp, base + H * k, qa, qb, h == 0, False)
-            wait("P", sgn[(k, h)])
-            ins = sums(k, T.Lh if byv else T.Lg, T.sg, base + H * k, qa, qb, False, h == 1)
-            if h == 1:
-                p_h[k] = sig(ins, "p_h%d" % k)
-
-        def x_mm(k, hs):
-            o = base + H * k
-            w = 64 * piece(k, hs[-1])[1]
-            wait("P", *[sgn[(k, h)] for h in hs])
-            P.matmul(X[k][:, 0:w], T.idp[:], T.sp[:, o:o + w], True, False)
-            if piece(k, hs[-1])[2]:
-                c = 64 * PA
-                P.matmul(X[k][:, 0:c], T.idn[:], T.sg[:, o:o + c], False, False)
-                ins = P.matmul(X[k][:, c:w], T.idh[:], T.sg[:, o + c:o + w], False, True)
-            else:
-                ins = P.matmul(X[k][:, 0:w], T.idn[:], T.sg[:, o:o + w], False, True)
-            p_x[k] = (sig(ins, "p_x%d" % k), w)
-
-        def x_out(k):
-            o = base + H * k
-            tok, w = p_x[k]
-            wait("A", tok)
-            a_x[k] = sig(A.activation(T.xs[:, o:o + w], X[k][:, 0:w], IDENT, bias=128.0), "a_x%d" % k)
-
-        def pass_on(k):
-            v_t[k] = turn(t, k, p_h[k])
-            if last:
-                return None
-            wait("g", v_t[k])
-            i = 2 * (t - 1) + k
-            return send(T.land[:, i, :], T.Tt[:, 2 * t + k, C:2 * C], "r_b%d" % i, "l_%d" % t)
-
-        offsets(0)
-        gather(0, 0)
-        finish(0, 0)
-        gather(0, 1)
-        finish(0, 1)
-        if tail or not final:
-            x_mm(0, (0, 1))
-        if tail:
-            x_out(0)
-        offsets(1)
-        gather(1, 0)
-        finish(1, 0)
-        if tail:
-            x_mm(1, (0,))
-            gather(1, 1)
-            x_out(1)
-            a, b = base + H + 64 * TW, base + S
-            wait("V", vg[(1, 1)])
-            v_m = sig(V.tensor_scalar(T.mm[:, 0:b - a], T.sp[:, a:b], 0.0, 256.0, AluOpType.is_lt, mul), "v_m")
-            wait("V", v_m)
-            v_x = sig(V.tensor_tensor(T.xs[:, a:b], T.sp[:, a:b], T.mm[:, 0:b - a], add), "v_x")
-            wait("D", a_x[0])
-            store(t * S, t * S + H)
-            wait("D", a_x[1], v_x)
-            store(t * S + H, (t + 1) * S)
-            break
-        pass_on(0)
-        gather(1, 1)
-        if final:
-            finish(1, 1)
+                a, b = base + H * k, base + H * k + H
+                calls[t, "X%d" % k] = ("P", every("s", [k]), lambda k=k, a=a, b=b: x_mm(X[k][:, 0:H], a, b))
+                calls[t, "x%d" % k] = ("A", [(t, "X%d" % k)], lambda k=k, a=a, b=b: x_out(X[k][:, 0:H], a, b))
+            if not tail:
+                calls[t, "T%d" % k] = ("V", every("a", [k]) + every("b", [k]), lambda k=k: turn(t, k))
+            if not last:
+                i = 2 * (t - 1) + k
+                calls[t, "r%d" % k] = ("g", [(t, "T%d" % k)], lambda k=k, i=i: send(
+                    T.land[:, i, :], T.Tt[:, 2 * t + k, C:2 * C], "r_b%d" % i, "l_%d" % t))
+            if not final:
+                calls.update(w_calls(t, k))
+            if t + 2 < M:
+                calls[t, "k%d" % k] = ("P", [(t, "T%d" % k)], lambda k=k: opening(k))
+        if not first:
+            calls.update(u_calls(t, 1, 2, (t, "u")))
+        if not final:
+            calls.update(s_calls(t, T.xs, base,
+                                 lambda k: every("G", [0, 1]) + [(t, ("m%d" if FUSE[k] else "x%d") % k)]))
             for k in range(2):
-                x_mm(k, (0, 1))
-                x_out(k)
-            left = pass_on(1)
-        else:
-            x_out(0)
-            wo, ws0 = w_ops(t, 0, 1, [v_t[0]])
-            wo[0]()
-            finish(1, 1)
-            x_mm(1, (0, 1))
-            x_out(1)
-            wo[1]()
-            wo[2]()
-            left = pass_on(1)
-            wo, ws1 = w_ops(t, 1, 2, [v_t[1]])
-            if first:
-                uo, us = u_ops(t + 1, 0, 2, [v_t[0], v_t[1], v_tc])
-            wait("V", ws0["c"], a_x[0], *vg.values())
-            for i in range(NP):
-                scatter(t, 0, T.xs, base, i)
-                if i < 3:
-                    wo[i]()
-                    if first:
-                        uo[i]()
-            wait("V", ws1["c"], a_x[1])
-            v_s = scatter(t, 1, T.xs, base)
+                if FUSE[k]:
+                    calls[t, "m%d" % k] = ("V", every("G", [k]),
+                                           lambda k=k: wrap(H * k, base + H * k, base + H * k + H))
+            calls.update(u_calls(t + 1, 0, 2 if first else 1, (t, "n")))
+            calls[t, "e"] = ("A", [("er", t + 1)], lambda: shift_e(t + 1))
             if not first:
-                a_hu = own_u(t + 1, [v_t[0], v_t[1], a_b2], T.bias2[:, 0:1])
-        wait("D", left)
+                calls.update(h_calls(t))
+        left = [] if last else [(t, "r1")]
         if first and t + 2 < M:
-            load_e(t + 2, t + 3)
-        if first and not final:
-            shift_e(t + 1)
-        if not first and t + 2 < M:
-            shift_e(t + 2)
-        if rank >= n - 2:
-            wait("D", a_x[0], a_x[1])
-            store(t * S, (t + 1) * S)
+            calls[t, "L"] = ("D", left, lambda: load_e(t + 2, t + 3))
+        xs = [(t, "x0"), (t, "x1")]
+        if tail:
+            calls[t, "Y0"] = ("D", xs[:1], lambda: store(t * S, t * S + H))
+            calls[t, "Y1"] = ("D", every("x", [1]), lambda: store(t * S + H, (t + 1) * S))
+        elif rank >= n - 2:
+            calls[t, "Y0"] = ("D", left + xs, lambda: store(t * S, (t + 1) * S))
         elif final:
-            wait("D", a_x[0], a_x[1])
-            store(S, M * S)
+            calls[t, "Y0"] = ("D", left + xs, lambda: store(S, M * S))
             if first:
-                store0()
+                calls[t, "Y1"] = ("D", [], store0)
+        emit({"V": named(t, V_TAIL if tail else V_FINAL if final else V_FIRST if first else V_NEXT),
+              "A": named(t, A_TAIL if tail else A_STEP),
+              "P": named(t, P_TAIL if tail else P_STEP), "g": named(t, "r0 r1"), "D": named(t, "L Y0 Y1")}, calls)
 
     for name in cnt:
         if done.get(name, 0) < cnt[name]:

@@ -1,27 +1,38 @@
 from concourse.mybir import AluOpType, ActivationFunctionType
 
 W, S, M = 8192, 768, 5
-H = S // 2
-C = H // 16
-Q = 6
 BIG = float(2 ** 20)
 MAGIC = 1.5 * 2 ** 26
 
-GP = {"first": ((2, 2, 2), (4, 2)), "next": ((2, 2, 2), (4, 2)), "final": ((2, 2, 2), (4, 2)),
+PART = (6, 6)
+GP = {"first": ((2, 2, 2), (2, 2, 2)), "next": ((2, 2, 2), (2, 2, 2)), "final": ((2, 2, 2), (2, 2, 2)),
       "tail": ((2, 2, 2), (2, 2, 2))}
-SP = ((2, 2, 2), (3, 3))
-FUSE = (True, False)
-V_ZERO = "T0 w00 T1 Tc w01 w10 n1 S00 w11 S01 S02 S10 n2 S11 S12"
-V_ZERO_NEXT = "T0 T1 w00 Tc w10 w01 w11 S00 S01 S02 S10 S11 S12 d n0 n1 n2"
-V_FIRST = "G00 G01 G02 G10 G11 G12 m0 T0 w00 w01 m1 T1 S00 w10 S01 n1 w11 S02 n2 S10 S11 S12"
-V_NEXT = "G00 u0 u1 G01 u2 G02 G10 G11 G12 T0 w00 m0 w01 m1 T1 S00 w10 S01 d w11 S02 S10 n0 n1 S11 n2 S12"
-V_FINAL = "G00 u0 u1 G01 u2 G02 G10 G11 G12 T0 T1"
-V_TAIL = "G00 u0 u1 G01 u2 G02 G10 G11 G12 m1 x11 x12"
-A_STEP = "s00 s01 s02 s10 s11 s12 e n0 r x1 h x0"
-A_TAIL = "s00 s01 s02 s10 s11 x0 x10 x11"
-P_STEP = "a00 a01 b00 a02 b01 b02 a10 a11 b10 a12 b11 b12 X1 X0 k0 k1"
-P_TAIL = "X0 X10 X11"
+MODE = {"first": ("FFD", "FFD"), "next": ("FFD", "FFD"), "final": ("SSD", "SSD"), "tail": ("SSS", "SSV")}
+SP = ((2, 2, 2), (4, 2))
+TB = (6, 12)
+ROUND = 1
+V_ZERO = "Tc L T0 w01 T1 S00 w10 S01 w11 n1 S02 n2 S10 S11"
+V_ZERO_NEXT = "Tc L T0 T1 w10 w01 w11 S00 S01 S02 S10 S11 n0 n2"
+V_FIRST = "G00 G01 G02 G11 G10 G12 T0 w00 w01 T1 S00 w10 S01 n1 w11 S02 n2 S11 S10"
+V_NEXT = "G00 u10 u11 G01 u12 G02 G10 G11 G12 T0 w00 w01 T1 S00 w10 S01 w11 S02 S10 n0 S11 n2"
+V_FINAL = "G00 u10 u11 G01 u12 G02 G10 G11 G12 T0 T1"
+V_TAIL = "G00 u10 u11 G01 u12 G02 G10 G11 G12 m12 x12"
+A_FIRST = "g02 g12 s00 s01 s11 s10 m00 m01 e x12 x02 m10 n0 m11"
+A_STEP = "g02 s00 s01 g12 s10 s11 m01 f0 m00 m10 m11 h0 x02 f1 x12 e h1"
+A_FINAL = "g02 s00 s01 g12 s10 s11 x10 x12 x02 x00"
+A_TAIL = "s00 s01 s02 x00 s10 s11 x01 x02 x10 x11"
+P_FIRST = "a00 a02 a01 b02 b00 b01 a12 a10 b11 b12 a11 b10 X02 X12 k1 k0"
+P_STEP = "a00 a02 a01 b00 b02 b01 a12 a10 a11 b10 b11 b12 d0 X02 X12 k0 o0 d1 k1 n1"
+P_FINAL = "a00 a02 a01 b00 b02 b01 a10 a11 a12 b12 b10 b11 X10 X02 X00 X12"
+P_TAIL = "X00 X01 X02 X10 X11"
+BYPE = (1, 1)
+EARLY = 2
+STEP = 1
+ADD = 1
+SPLIT = "PP"
+LAST = 0
 
+NK = 4
 SCRATCH = {
     "tb": ("sbuf", [128, W], "bfloat16"),
     "er": ("sbuf", [128, M * S], "bfloat16"),
@@ -29,42 +40,41 @@ SCRATCH = {
     "sp": ("sbuf", [128, 4 * S], "bfloat16"),
     "sg": ("sbuf", [128, 4 * S], "bfloat16"),
     "xs": ("sbuf", [128, 4 * S], "bfloat16"),
-    "mm": ("sbuf", [128, S], "bfloat16"),
+    "mm": ("sbuf", [128, 4 * S], "bfloat16"),
     "hws": ("sbuf", [128, 16], "bfloat16"),
     "Ls": ("sbuf", [128, 2, 160], "bfloat16"),
     "Lg": ("sbuf", [128, 2, 160], "bfloat16"),
+    "Lc": ("sbuf", [128, 2, 160], "bfloat16"),
     "Gp": ("sbuf", [128, 2, 4], "bfloat16"),
     "one8": ("sbuf", [128, 2, 4], "bfloat16"),
     "ones": ("sbuf", [128, 128], "bfloat16"),
-    "negs": ("sbuf", [128, 128], "bfloat16"),
+    "idf": ("sbuf", [128, 128], "float32"),
+    "idm": ("sbuf", [128, 128], "bfloat16"),
     "idp": ("sbuf", [128, 128], "bfloat16"),
     "idn": ("sbuf", [128, 128], "bfloat16"),
-    "c128": ("sbuf", [128, 16], "bfloat16"),
-    "Kc": ("sbuf", [128, 2, 4, 32], "bfloat16"),
-    "Kr": ("sbuf", [128, 64], "bfloat16"),
-    "Tt": ("sbuf", [128, 2 * M, 128], "float32"),
+    "idh": ("sbuf", [128, 128], "bfloat16"),
+    "c128": ("sbuf", [128, 32], "bfloat16"),
+    "Kc": ("sbuf", [128, NK, 4, 32], "bfloat16"),
+    "Kr": ("sbuf", [128, 2, 64], "bfloat16"),
+    "Tt": ("sbuf", [128, NK * M, 128], "float32"),
     "Tc": ("sbuf", [128, 32], "float32"),
     "cvin": ("sbuf", [128, 8], "float32"),
     "col": ("sbuf", [128, 8], "float32"),
-    "land": ("sbuf", [128, 8, C], "float32"),
-    "ru": ("sbuf", [128, 8, C], "bfloat16"),
-    "du": ("sbuf", [128, 8, C], "float32"),
-    "h1": ("sbuf", [128, 8, C], "float32"),
-    "h2": ("sbuf", [128, 8, C], "float32"),
-    "hr": ("sbuf", [128, 8, C], "bfloat16"),
-    "ha": ("sbuf", [128, 8, C], "float32"),
-    "offu": ("sbuf", [128, 8, C], "uint16"),
-    "rw": ("sbuf", [128, 8, C], "float32"),
-    "offw": ("sbuf", [128, 8, C], "uint16"),
-    "R0": ("psum", [128, 2, 512], "float32"),
-    "R1": ("psum", [128, 2, 512], "float32"),
-    "RC": ("psum", [128, 2, 512], "float32"),
-    "X0": ("psum", [128, 512], "float32"),
-    "X1": ("psum", [128, 512], "float32"),
+    "land": ("sbuf", [128, 4 * NK, 32], "float32"),
+    "ru": ("sbuf", [128, 4 * NK, 32], "bfloat16"),
+    "du": ("sbuf", [128, 4 * NK, 32], "float32"),
+    "h1": ("sbuf", [128, 4 * NK, 32], "float32"),
+    "h2": ("sbuf", [128, 4 * NK, 32], "float32"),
+    "hr": ("sbuf", [128, 4 * NK, 32], "bfloat16"),
+    "ha": ("sbuf", [128, 4 * NK, 32], "float32"),
+    "offu": ("sbuf", [128, 4 * NK, 32], "uint16"),
+    "rw": ("sbuf", [128, 4 * NK, 32], "float32"),
+    "offw": ("sbuf", [128, 4 * NK, 32], "uint16"),
+    "PS": ("psum", [128, 8, 8, 64], "float32"),
 }
 SEMAPHORES = (
-    ["V", "A", "P", "g", "d_hw", "d_e0", "d_e1", "d_e2", "d_e3", "d_e4", "d_t0", "d_t1", "d_t2", "d_y"]
-    + ["r_c", "l_c"] + ["r_b%d" % i for i in range(8)] + ["l_%d" % t for t in range(1, M)]
+    ["V", "A", "P", "g", "d_hw", "d_e0", "d_e1", "d_f1", "d_e2", "d_e3", "d_e4", "d_y", "d_y1", "d_y2", "d_y3", "d_y4", "g_y"] + ["d_t%d" % i for i in range(6)]
+    + ["r_c", "l_c"] + ["r_b%d" % i for i in range(4 * NK)] + ["l_%d" % t for t in range(1, M)]
 )
 
 
@@ -82,6 +92,9 @@ def rank_program(g, core, T, topo):
     queue = {"V": V, "A": A, "P": P, "D": D, "g": g}
     add, sub, mul = AluOpType.add, AluOpType.subtract, AluOpType.mult
     IDENT, SIGN = ActivationFunctionType.Identity, ActivationFunctionType.Sign
+    K, Q = len(PART), max(PART)
+    C = 4 * Q
+    at = [64 * a for a, _ in cuts(PART)]
     cnt, seen, done = {}, {}, {}
 
     def sig(ins, name, k=1):
@@ -121,11 +134,12 @@ def rank_program(g, core, T, topo):
     if not last:
         nxt = T.cores[rank + 1]
         rid, pid, _ = topo.addr(nxt)
-        omask, oeng = topo.mask(core, nxt), len(topo.engines(core, nxt))
+        some = topo.engines(core, nxt)[::STEP]
+        omask, oeng = sum(1 << e for e in some), len(some)
     if not first:
-        ieng = len(topo.engines(T.cores[rank - 1], core))
+        ieng = len(topo.engines(T.cores[rank - 1], core)[::STEP])
         tok["cv"] = owe("r_c", ieng)
-        for i in range(8):
+        for i in range(4 * K):
             tok["land", i] = owe("r_b%d" % i, ieng)
 
     def send(dst, src, rsem, lsem):
@@ -144,14 +158,22 @@ def rank_program(g, core, T, topo):
         tok["tb", i] = sig(D.dma_start(T.tb[:, a:b], T.tab[:, a:b]), "d_t%d" % i, 16)
 
     load_e(0, 1)
-    load_t(0, 0, 8 * H)
-    load_t(1, 8 * H, 8 * S)
-    load_e(1, 2)
-    load_t(2, 8 * S, W)
+    for i, b in enumerate(TB):
+        load_t(i, 512 * (TB[i - 1] if i else 0), 512 * b)
+    def load_first(k0, k1, name):
+        a, b = S + at[k0], S + (at + [S])[k1]
+        d = sig(D.dma_start(T.er[:, a:b], T.res[:, a:b]), name, 16)
+        for k in range(k0, k1):
+            tok["er", 1, k] = d
+
+    load_first(0, EARLY, "d_e1")
+    load_t(len(TB), 8 * S, W)
+    if EARLY < K:
+        load_first(EARLY, K, "d_f1")
     load_e(2, 3 if first else M)
 
-    def store(a, b):
-        return sig(D.dma_start(T.y[:, a:b], T.xs[:, a - S:b - S]), "d_y", 16)
+    def store(a, b, name="d_y"):
+        return sig(D.dma_start(T.y[:, a:b], T.xs[:, a - S:b - S]), name, 16)
 
     def store0():
         wait("D", tok["er", 0])
@@ -160,156 +182,279 @@ def rank_program(g, core, T, topo):
     if not first:
         store0()
 
-    def iota(out, pattern):
-        return g.iota(out, pattern, 0, 0, allow_small_or_imprecise_dtypes=True)
-
     v_one8 = sig(V.memset(T.one8[:], 1.0), "V")
     v_kc = sig(V.memset(T.Kc[0:64], 0.0), "V")
-    wait("g", v_one8, sig(iota(T.Kr[32:64, :], [[8, 64]]), "g"))
+    g_kr = sig(g.iota(T.Kr[0:32], [[0, 2], [8, 64]], 0, 0, allow_small_or_imprecise_dtypes=True), "g")
+    wait("g", v_one8)
     g0 = sig(g.affine_select(T.Gp[:], T.one8[:], [[-16, 2], [-32, 4]], AluOpType.is_ge, 0.0, 0, 1), "g")
-    wait("g", v_kc)
-    for k in range(2):
-        if len(set(SP[k])) == 1:
-            iota(T.Kc[0:1, k, :, 3 * Q:4 * Q], [[0, 4], [0, len(SP[k])], [512, SP[k][0]]])
-        else:
-            for a, b in cuts(SP[k]):
-                iota(T.Kc[0:1, k, :, 3 * Q + a:3 * Q + b], [[0, 4], [512, b - a]])
     wait("g", g0)
     g1 = sig(g.affine_select(T.Gp[:], T.Gp[:], [[16, 2], [32, 4]], AluOpType.is_ge, 0.0, 15, -1), "g")
     V.memset(T.Ls[:], 0.0)
-    V.memset(T.Lg[:], 0.0)
-    V.memset(T.ones[:], 1.0)
-    v_ones = sig(V.memset(T.negs[:], -128.0), "V")
+    v_ones = sig(V.memset(T.ones[:], 1.0), "V")
+    V.memset(T.Kr[32:64], 1.0)
     wait("V", v_kc)
-    V.memset(T.Kc[0:1, :, :, 2 * Q:3 * Q], -3.5)
-    V.memset(T.Kc[32:33, :, :, 3 * Q:4 * Q], 1.0)
-    V.memset(T.Kr[0:32, :], 1.0)
-    v_z = sig(V.memset(T.c128[:], 128.0), "V")
+    V.memset(T.Kc[32:33, 0:K, :, 2 * Q:3 * Q], -3.5)
+    V.memset(T.Kc[0:1, 0:K, :, 3 * Q:4 * Q], 1.0)
+    for k in range(K):
+        step = SP[k][0] if len(set(SP[k])) == 1 else Q
+        for a, b in cuts(SP[k])[:1 if step < Q else None]:
+            for q in range(a + 1, b):
+                V.memset(T.Kc[32:33, k, :, 3 * Q + q:4 * Q:step], 512.0 * (q - a))
+    V.memset(T.Kc[32:33, K, :, 2 * Q:3 * Q], MAGIC)
+    v_z = sig(V.memset(T.Kc[32:33, K + 1, :, 2 * Q:3 * Q], -MAGIC), "V")
+    v_l = sig(V.memset(T.c128[:], 128.0), "V")
     wait("g", v_ones)
-    for o, b in ((T.idp, T.ones), (T.idn, T.negs)):
-        tok["id"] = sig(g.affine_select(o[:], b[:], [[-1, 128]], AluOpType.is_equal, 0.0, 0, 1), "g")
-    wait("V", v_z, g1, d_hw)
-    for L, kinds, scale in ((T.Ls, (2, 3, 0, 1), 1.0), (T.Lg, (0, 1), -128.0)):
+    for o, c in ((T.idp, 1.0), (T.idf, 1.0)):
+        tok["id"] = sig(g.affine_select(o[:], T.ones[:], [[-1, 128]], AluOpType.is_equal, 0.0, 0, 1), "g")
+
+    def weights(L, kinds, scale):
         for kind in kinds:
-            o, w = 5 + Q * kind, min(kind, 2)
+            o, w = Q - 1 + Q * kind, min(kind, 2)
             ins = V.tensor_scalar(L[:, :, o:o + 128:32], T.Gp[:], T.hws[:, w:w + 1], scale, mul, mul)
-        tok[L.name] = sig(ins, "V")
-
-    R = [T.R0, T.R1]
-    X = [T.X0, T.X1]
-
-    def opening(k):
-        for par in range(2):
-            ins = P.matmul(R[k][:, par, 0:64], T.Kc[0:64, k], T.Kr[0:64, :], True, False)
         return ins
 
-    def sums(k, L, src, base, q0, q1, start, stop):
-        ins = None
+    wait("V", v_ones, g1, d_hw)
+    tok["Ls"] = sig(weights(T.Ls, (2, 3, 0, 1), 1.0), "V")
+    V.memset(T.Lg[:], 0.0)
+    tok["L0"] = sig(V.memset(T.Lc[:], 0.0), "V")
+    wait("A", tok["id"])
+    for o, c in ((T.idm, -1.0), (T.idn, -128.0), (T.idh, -256.0)):
+        tok["ids"] = sig(A.activation(o[:], T.idp[:], IDENT, scale=c), "A")
+
+    def role(t):
+        return ("tail" if last else "final") if t == M - 1 else "first" if first else "next"
+
+    def pieces(t, k):
+        return [(h, qa, qb, MODE[role(t)][k][h]) for h, (qa, qb) in enumerate(cuts(GP[role(t)][k]))]
+
+    def opening(k, t):
+        ins = P.matmul(T.PS[:, k, 0:2, :], T.Kc[0:64, k], T.Kr[0:64], True, False)
+        for h, qa, qb, mode in pieces(t, k) if t else []:
+            if mode in "DA":
+                ins = sums(k, T.Ls, T.er, t * S + at[k], qa, qb, False)
+        return ins
+
+    def sums(k, L, src, base, q0, q1, stop):
         for q in range(q0, q1):
             for par in range(2):
-                ins = P.matmul(R[k][:, par, 0:64], L[:, par, 5 - q:133 - q], src[:, base + 64 * q:base + 64 * q + 64],
-                               start and q == q0, stop and q == q1 - 1)
+                ins = P.matmul(T.PS[:, k, par, :], L[:, par, Q - 1 - q:Q + 127 - q],
+                               src[:, base + 64 * q:base + 64 * q + 64], False, stop and q == q1 - 1 and par == 1)
         return ins
 
     def turn(t, k):
         for b in range(4):
-            ins = V.transpose(T.Tt[:, 2 * t + k, b:128:4], R[k][:, :, 16 * b:16 * b + 16])
+            ins = V.transpose(T.Tt[:, K * t + k, b:128:4], T.PS[:, k, 0:2, 16 * b:16 * b + 16])
         return ins
 
     def w_calls(t, k):
-        i = 2 * t + k
+        i = K * t + k
+        if t == 0 and k < ROUND:
+            return {(t, "w%d1" % k): ("V", [(t, "T%d" % k)], lambda: V.tensor_tensor(
+                T.offw[:, i, 0:C], T.Tt[:, i, 3 * C:4 * C], T.Tt[:, i, 2 * C:3 * C], sub))}
         return {
             (t, "w%d0" % k): ("V", [(t, "T%d" % k)], lambda: V.tensor_scalar(
-                T.rw[:, i, :], T.Tt[:, i, 2 * C:3 * C], MAGIC, MAGIC, add, sub)),
+                T.rw[:, i, 0:C], T.Tt[:, i, 2 * C:3 * C], MAGIC, MAGIC, add, sub)),
             (t, "w%d1" % k): ("V", [(t, "w%d0" % k)], lambda: V.tensor_tensor(
-                T.offw[:, i, :], T.Tt[:, i, 3 * C:4 * C], T.rw[:, i, :], sub)),
+                T.offw[:, i, 0:C], T.Tt[:, i, 3 * C:4 * C], T.rw[:, i, 0:C], sub)),
         }
 
     def u_calls(t, k0, k1, name):
-        a, b = 2 * (t - 1) + k0, 2 * (t - 1) + k1
+        a, b = K * (t - 1) + k0, K * (t - 1) + k1
         s, c = name
+        hr, ha = T.hr[:, a:b, 0:C], T.ha[:, a:b, 0:C]
         if first:
-            deps = [(t - 1, "T0"), (t - 1, "T1"), "col"]
+            deps = [(t - 1, "T%d" % k) for k in range(K)] + ["col"]
             lo, hi = (BIG + W - 4095.5, BIG + W) if t == 1 else (T.col[:, 0:1], T.col[:, 1:2])
-            calls = {(s, c + "0"): ("A", deps, lambda: A.activation(T.hr[:, a:b, :], T.Tt[:, a:b, 0:C], IDENT, bias=lo)),
-                     (s, c + "1"): ("V", deps, lambda: V.tensor_scalar(T.ha[:, a:b, :], T.Tt[:, a:b, 0:C], hi, None, add))}
+            calls = {(s, c + "0"): ("A", deps, lambda: A.activation(hr, T.Tt[:, a:b, 0:C], IDENT, bias=lo)),
+                     (s, c + "1"): ("V", deps, lambda: V.tensor_scalar(ha, T.Tt[:, a:b, 0:C], hi, None, add))}
         else:
-            deps = [(t - 1, "h"), ("land", a)]
-            calls = {(s, c + "0"): ("V", deps, lambda: V.tensor_tensor(T.hr[:, a:b, :], T.h1[:, a:b, :], T.land[:, a:b, :], add)),
-                     (s, c + "1"): ("V", deps, lambda: V.tensor_tensor(T.ha[:, a:b, :], T.h2[:, a:b, :], T.land[:, a:b, :], add))}
-        calls[s, c + "2"] = ("V", [(s, c + "0"), (s, c + "1")], lambda: V.tensor_tensor(
-            T.offu[:, a:b, :], T.ha[:, a:b, :], T.hr[:, a:b, :], sub))
+            deps = [(t - 1, "h%d" % k0 if SPLIT else "h"), ("land", a)]
+            land = T.land[:, a:b, 0:C]
+            calls = {(s, c + "0"): ("V", deps, lambda: V.tensor_tensor(hr, T.h1[:, a:b, 0:C], land, add)),
+                     (s, c + "1"): ("V", deps, lambda: V.tensor_tensor(ha, T.h2[:, a:b, 0:C], land, add))}
+            if k0 < BYPE[1]:
+                ha = T.PS[:, 7 - k0, 0, 0:C]
+                calls[s, c + "1"] = ("P", [(t - 1, "o%d" % k0), ("land", a)],
+                                     lambda: P.matmul(ha, T.idf[:], T.land[:, a, 0:C], False, True))
+        calls[s, c + "2"] = ("V", [(s, c + "0"), (s, c + "1")], lambda: V.tensor_tensor(T.offu[:, a:b, 0:C], ha, hr, sub))
         return calls
+
+    def held(mode):
+        return T.xs if mode == "F" and ADD else T.sp
+
+    def under(t, k, qa, qb):
+        over = [(h, mode) for h, pa, pb, mode in pieces(t, k) if pa < qb and qa < pb]
+        return [h for h, _ in over], all(mode == "F" for _, mode in over)
 
     def s_calls(t, src, base, deps):
         calls = {}
-        for k in range(2):
-            for i, (a, b) in enumerate(cuts(SP[k])):
-                def scatter(k=k, a=a, b=b):
-                    win = T.tb[:, 8 * H * k + 512 * a:8 * H * k + 512 * b].indirect(T.offw[:, 2 * t + k, 4 * a:4 * b])
-                    o = base + H * k
-                    if t and FUSE[k]:
-                        return V.tensor_tensor(win, T.sp[:, o + 64 * a:o + 64 * b],
-                                               T.mm[:, H * k + 64 * a:H * k + 64 * b], add)
-                    return V.tensor_copy(win, src[:, o + 64 * a:o + 64 * b])
-                calls[t, "S%d%d" % (k, i)] = ("V", [(t, "w%d1" % k)] + deps(k), scatter)
+        for k in range(K):
+            for i, (qa, qb) in enumerate(cuts(SP[k])):
+                def scatter(k=k, qa=qa, qb=qb):
+                    a, b = at[k] + 64 * qa, at[k] + 64 * qb
+                    win = T.tb[:, 8 * a:8 * b].indirect(T.offw[:, K * t + k, 4 * qa:4 * qb])
+                    if t and under(t, k, qa, qb)[1]:
+                        return V.tensor_tensor(win, held("F")[:, base + a:base + b], T.mm[:, base + a:base + b], add)
+                    return V.tensor_copy(win, src[:, base + a:base + b])
+                calls[t, "S%d%d" % (k, i)] = ("V", [(t, "w%d1" % k)] + deps(k, qa, qb), scatter)
         return calls
 
-    def x_mm(bank, a, b):
-        P.matmul(bank, T.idp[:], T.sp[:, a:b], True, False)
-        return P.matmul(bank, T.idn[:], T.sg[:, a:b], False, True)
+    free = {}
 
-    def x_out(bank, a, b):
-        return A.activation(T.xs[:, a:b], bank, IDENT, bias=128.0)
+    def units(t, k):
+        out = []
+        for h, qa, qb, mode in pieces(t, k):
+            if out and out[-1][3] == mode != "A" and role(t) != "tail":
+                out[-1][0].append(h)
+                out[-1][2] = qb
+            elif mode != "V" and not (mode == "F" and ADD):
+                out.append([[h], qa, qb, mode])
+        return out
+
+    def x_calls(t, k, j, hs, a, b, mode):
+        i = K + j + sum(len(units(t, p)) for p in range(k))
+        assert i < 8 - max(BYPE) or first or role(t) == "tail"
+        bank, kh, calls = T.PS[:, i, 0:(b - a) // 64, :], "%d%d" % (k, hs[0]), {}
+
+        def x_mm(whole):
+            if mode in "DA":
+                P.matmul(bank, T.idp[:], T.er[:, S + a:S + b], True, False)
+            ins = P.matmul(bank, T.idp[:], T.sp[:, a:b], mode not in "DA", not whole)
+            return P.matmul(bank, T.idh[:] if mode == "D" else T.idn[:], T.sg[:, a:b], False, True) if whole else ins
+
+        if mode == "A":
+            calls[t, "z" + kh] = ("P", free.get(i, []) + [("er", t) if t > 1 else ("er", t, k)],
+                                  lambda: P.matmul(bank, T.idp[:], T.er[:, S + a:S + b], True, False))
+            calls[t, "Z" + kh] = ("P", [(t, "g" + kh)], lambda: P.matmul(bank, T.idp[:], T.sp[:, a:b], False, True))
+            calls[t, "s" + kh] = ("A", [(t, "Z" + kh)], lambda: A.activation(T.sg[:, a:b], bank, SIGN, bias=0.5))
+        deps = [(t, "%s%d%d" % (c, k, h)) for h in hs for c in ("gG" if mode == "D" else "s")]
+        if i >= 6 and not first:
+            deps.append((t, "u12"))
+        calls[t, "X" + kh] = ("P", deps + free.get(i, []), lambda: x_mm(True))
+        calls[t, "x" + kh] = ("A", [(t, "X" + kh)], lambda: A.activation(T.xs[:, a:b], bank, IDENT, bias=128.0))
+        free[i] = [(t, "x" + kh)]
+        return calls
 
     def wrap(o, a, b):
         return V.tensor_scalar(T.mm[:, o:o + b - a], T.sp[:, a:b], 0.0, 256.0, AluOpType.is_lt, mul)
 
-    def shift_e(t):
-        return A.activation(T.ep[:, (t - 1) * S:t * S], T.er[:, t * S:(t + 1) * S], IDENT, bias=-256.0)
+    def shift_e(t, ks):
+        spans = []
+        for k in ks:
+            for h, qa, qb, mode in pieces(t, k):
+                a, b = at[k] + 64 * qa, at[k] + 64 * qb
+                if mode != "A" and spans and spans[-1][1:] == [a, mode == "D"]:
+                    spans[-1][1] = b
+                elif mode != "A":
+                    spans.append([a, b, mode == "D"])
+        for a, b, dual in spans:
+            ins = A.activation(T.ep[:, (t - 1) * S + a:(t - 1) * S + b], T.er[:, t * S + a:t * S + b],
+                               IDENT, bias=255.0 if dual else -256.0, scale=-1.0 if dual else 1.0)
+        return ins
 
     def h_calls(t):
-        a, b = 2 * t, 2 * t + 2
-        u = T.Tt[:, a:b, 0:C]
+        if not SPLIT:
+            return h_all(t)
+        calls = {}
+        up, lo, hi = ((T.col[:, 0:1], T.col[:, 3:4], T.col[:, 4:5]) if t else (BIG + 0.5, T.col[:, 1:2], T.col[:, 2:3]))
+        for k in range(K):
+            i = K * t + k
+            u, ru = T.Tt[:, i, 0:C], T.ru[:, i, 0:C]
+            du = T.PS[:, 7 - k, 0, 0:C] if SPLIT[k] == "P" else T.du[:, i, 0:C]
+
+            def minus(u=u, ru=ru, du=du, k=k):
+                if SPLIT[k] == "V":
+                    return V.tensor_tensor(du, u, ru, sub)
+                P.matmul(du, T.idf[:], u, True, False)
+                return P.matmul(du, T.idm[:], ru, False, True)
+
+            def both(i=i, du=du):
+                A.activation(T.h1[:, i, 0:C], du, IDENT, bias=lo)
+                return A.activation(T.h2[:, i, 0:C], du, IDENT, bias=hi)
+
+            calls[t, "f%d" % k] = ("A", [(t, "T%d" % k), "col"], lambda u=u, ru=ru: A.activation(ru, u, IDENT, bias=up))
+            calls[t, "d%d" % k] = (SPLIT[k], [(t, "f%d" % k), "ids", "Tc"], minus)
+            calls[t, "h%d" % k] = ("A", [(t, "d%d" % k), "col2" if t else "col1"], both)
+            if k < BYPE[1]:
+                calls[t, "o%d" % k] = ("P", [(t, "h%d" % k)], lambda k=k, i=i: P.matmul(
+                    T.PS[:, 7 - k, 0, 0:C], T.idf[:], T.h2[:, i, 0:C], True, False))
+        return calls
+
+    def h_all(t):
+        a, b = K * t, K * t + K
+        u, du = T.Tt[:, a:b, 0:C], T.du[:, a:b, 0:C]
         up, lo, hi = ((T.col[:, 0:1], T.col[:, 3:4], T.col[:, 4:5]) if t else (BIG + 0.5, T.col[:, 1:2], T.col[:, 2:3]))
 
         def both():
-            A.activation(T.h1[:, a:b, :], T.du[:, a:b, :], IDENT, bias=lo)
-            return A.activation(T.h2[:, a:b, :], T.du[:, a:b, :], IDENT, bias=hi)
+            A.activation(T.h1[:, a:b, 0:C], du, IDENT, bias=lo)
+            return A.activation(T.h2[:, a:b, 0:C], du, IDENT, bias=hi)
 
-        return {(t, "r"): ("A", [(t, "T0"), (t, "T1"), "col"], lambda: A.activation(T.ru[:, a:b, :], u, IDENT, bias=up)),
-                (t, "d"): ("V", [(t, "r")], lambda: V.tensor_tensor(T.du[:, a:b, :], u, T.ru[:, a:b, :], sub)),
-                (t, "h"): ("A", [(t, "d"), "col2"], both)}
+        calls = {(t, "r"): ("A", [(t, "T%d" % k) for k in range(K)] + ["col"],
+                            lambda: A.activation(T.ru[:, a:b, 0:C], u, IDENT, bias=up)),
+                 (t, "d"): ("V", [(t, "r")], lambda: V.tensor_tensor(du, u, T.ru[:, a:b, 0:C], sub)),
+                 (t, "h"): ("A", [(t, "d"), "col2"], both)}
+        if BYPE[0]:
+            du = T.PS[:, 7, 0:K, 0:C]
+
+            def minus():
+                P.matmul(du, T.idf[:], u, True, False)
+                return P.matmul(du, T.idm[:], T.ru[:, a:b, 0:C], False, True)
+
+            calls[t, "d"] = ("P", [(t, "r"), "ids", "Tc"], minus)
+        for k in range(BYPE[1]):
+            calls[t, "o%d" % k] = ("P", [(t, "h")], lambda k=k: P.matmul(
+                T.PS[:, 7 - k, 0, 0:C], T.idf[:], T.h2[:, a + k, 0:C], True, False))
+        return calls
+
+    if ADD:
+        wait("A", tok["er", 0])
+        for t in range(1, M - 1):
+            for k in range(K):
+                for hs, qa, qb, mode in units(t, k):
+                    a, b = (t - 1) * S + at[k] + 64 * qa, (t - 1) * S + at[k] + 64 * qb
+                    tok["zero"] = sig(A.activation(T.mm[:, a:b], T.er[:, 0:b - a], IDENT, scale=0.0), "A")
 
     def named(t, order):
         return [c if c in ("Tc", "pc", "cs", "col", "col1", "col2") else (t, c) for c in order.split()]
 
-    calls = {(0, "e"): ("A", [("er", 1)], lambda: shift_e(1))}
-    wait("P", v_z, g1)
-    for k in range(2):
-        opening(k)
-        calls[0, "b%d" % k] = ("P", ["Ls", ("er", 0)], lambda k=k: sums(k, T.Ls, T.er, H * k, 0, Q, False, True))
+    calls = {(0, "e%d" % k): ("A", [("er", 1, k)], lambda k=k: shift_e(1, [k])) for k in range(EARLY if first else K)}
+    wait("P", v_z, g_kr)
+    for k in range(K):
+        opening(k, 0)
+
+        def zero(k=k):
+            ins = sums(k, T.Ls, T.er, at[k], 0, PART[k], k >= ROUND)
+            for i in range(2 * (k < ROUND)):
+                ins = P.matmul(T.PS[:, k, 0:2, :], T.Kc[0:64, K + i], T.Kr[0:64], False, i == 1)
+            return ins
+
+        calls[0, "b%d" % k] = ("P", ["Ls", ("er", 0)], zero)
         calls[0, "T%d" % k] = ("V", [(0, "b%d" % k)], lambda k=k: turn(0, k))
-        calls[0, "k%d" % k] = ("P", [(0, "T%d" % k)], lambda k=k: opening(k))
+        if k < EARLY or not first:
+            calls[0, "k%d" % k] = ("P", [(0, "T%d" % k), ("er", 1, k)], lambda k=k: opening(k, 1))
         calls.update(w_calls(0, k))
 
     def const_sums():
         for par in range(2):
-            ins = P.matmul(T.RC[:, par, 0:16], T.Ls[:, par, 5:133], T.c128[:], True, True)
+            ins = P.matmul(T.PS[:, 6 + par, 0, 0:16], T.Ls[:, par, Q - 1:Q + 127], T.c128[:, 0:16], True, True)
         return ins
 
     def column(i, src, bias):
         return A.activation(T.col[:, i:i + 1], src, IDENT, bias=bias)
 
     cu, cv = T.Tc[:, 0:1], T.cvin[:, 0:1]
-    calls["pc"] = ("P", [], const_sums)
-    calls["Tc"] = ("V", ["pc"], lambda: V.transpose(T.Tc[:], T.RC[:, :, 0:16]))
-    calls.update(s_calls(0, T.er, 0, lambda k: [("tb", k)]))
+    tok["c128"] = v_l
+    calls[0, "L"] = ("V", ["L0"], lambda: [weights(T.Lg, (0, 1), -128.0), weights(T.Lc, (0, 1), -256.0)][1])
+    calls["pc"] = ("P", ["c128", "Ls"], const_sums)
+    calls["Tc"] = ("V", ["pc"], lambda: V.transpose(T.Tc[:], T.PS[:, 6:8, 0, 0:16]))
+    free[6] = free[7] = ["Tc"]
+    calls.update(s_calls(0, T.er, 0, lambda k, qa, qb: [("tb", i) for i in range(len(TB))
+                                                         if (TB[i - 1] if i else 0) < at[k] // 64 + qb]))
     if not last:
         calls["cs"] = ("g", ["Tc"], lambda: send(T.cvin[:, 0:1], T.Tc[:, Q:Q + 1], "r_c", "l_c"))
     if first:
         tok["col"] = tok["Ls"]
-        calls.update(u_calls(1, 0, 2, (0, "n")))
+        calls.update(u_calls(1, 0, K, (0, "n")))
         calls["col1"] = ("A", ["Tc"], lambda: [column(0, cu, BIG + W - 4095.5), column(1, cu, BIG + W)][1])
     else:
         calls.update(u_calls(1, 0, 1, (0, "n")))
@@ -317,94 +462,121 @@ def rank_program(g, core, T, topo):
         calls["col"] = ("A", ["Tc"], lambda: column(0, cu, BIG + 0.5))
         calls["col1"] = ("A", ["cv"], lambda: [column(1, cv, 2 * BIG + W - 4095.5), column(2, cv, 2 * BIG + W)][1])
         calls["col2"] = ("A", ["col1"], lambda: [column(3, cu, T.col[:, 1:2]), column(4, cu, T.col[:, 2:3])][1])
-    emit({"P": named(0, "b0 b1 pc k0 k1"), "V": named(0, V_ZERO if first else V_ZERO_NEXT), "g": ["cs"],
-          "A": named(0, "n0 col r e col1 col2 h")}, calls)
+    emit({"P": named(0, "pc b0 b1 k0 k1 d d0 d1 o0 o1 n1"), "V": named(0, V_ZERO if first else V_ZERO_NEXT), "g": ["cs"],
+          "A": named(0, "n0 col r f0 f1 e0 e1 col1 h0 h1 col2 h")}, calls)
     if first:
         tok["col"] = tok["col1"]
-    wait("P", tok["Lg"], tok["id"])
+    wait("P", tok[0, "L"], tok["ids"])
 
     for t in range(1, M):
         final = t == M - 1
         tail = final and last
         base = (t - 1) * S
         calls = {}
-        table = [(t - 1, "S%d%d" % (k, i)) for k in range(2) for i in range(len(SP[k]))] + [("tb", 2), (t - 1, "e")]
-        gp = GP["tail" if tail else "final" if final else "first" if first else "next"]
-        every = lambda c, ks: [(t, "%s%d%d" % (c, k, h)) for k in ks for h in range(len(gp[k]))]
-        issued = {0: [], 1: []}
+        table = [(t - 1, "S%d%d" % (k, i)) for k in range(K) for i in range(len(SP[k]))] + [("tb", len(TB))]
+        every = lambda c, ks=range(K): [x for x in calls if x[1][0] == c and int(x[1][1]) in ks]
+        issued = {k: [] for k in range(K)}
 
         def part(k, L, src, qa, qb):
             issued[k].append(qa)
-            return sums(k, L, src, base + H * k, qa, qb, final and len(issued[k]) == 1, len(issued[k]) == 2 * len(gp[k]))
+            return sums(k, L, src, base + at[k], qa, qb, len(issued[k]) == 2 * len(pieces(t, k)))
 
-        for k in range(2):
-            for h, (qa, qb) in enumerate(cuts(gp[k])):
-                a, b = base + H * k + 64 * qa, base + H * k + 64 * qb
+        for k in range(K):
+            shifted, opened = (t - 1, "e" if t > 1 else "e%d" % k), []
+            if first and t == 1 and k >= EARLY:
+                shifted, opened = (t, "E%d" % k), [(t, "O%d" % k)]
+                calls[shifted] = ("A", [("er", 1, k)], lambda k=k: shift_e(1, [k]))
+                calls[opened[0]] = ("P", [(0, "T%d" % k), ("er", 1, k)], lambda k=k: opening(k, 1))
+            for h, qa, qb, mode in pieces(t, k):
+                a, b = base + at[k] + 64 * qa, base + at[k] + 64 * qb
                 kh = "%d%d" % (k, h)
-                off = (t - 1, "n2") if first or k == 0 else (t, "u2")
-                calls[t, "G" + kh] = ("V", table + [off], lambda k=k, qa=qa, qb=qb, a=a, b=b: V.tensor_tensor(
-                    T.sp[:, a:b], T.tb[:, 0:W].indirect(T.offu[:, 2 * (t - 1) + k, 4 * qa:4 * qb]), T.ep[:, a:b], add))
-                calls[t, "s" + kh] = ("A", [(t, "G" + kh)], lambda a=a, b=b: A.activation(
-                    T.sg[:, a:b], T.sp[:, a:b], SIGN, bias=0.5))
+                ready = table + [(t - 1, "n2") if first or k == 0 else (t, "u%d2" % k)]
+                slots = T.tb[:, 0:W].indirect(T.offu[:, K * (t - 1) + k, 4 * qa:4 * qb])
+                if mode != "A":
+                    out, op = (T.sg, AluOpType.is_gt) if mode == "D" else (held(mode), add)
+                    calls[t, "G" + kh] = ("V", ready + [shifted], lambda a=a, b=b, slots=slots, out=out, op=op:
+                                          V.tensor_tensor(out[:, a:b], slots, T.ep[:, a:b], op))
+                if mode in "SF":
+                    calls[t, "s" + kh] = ("A", [(t, "G" + kh)], lambda a=a, b=b, mode=mode: A.activation(
+                        T.sg[:, a:b], held(mode)[:, a:b], SIGN, bias=0.5))
+                if mode in "DA":
+                    calls[t, "g" + kh] = ("A", ready, lambda a=a, b=b, slots=slots, mode=mode: A.activation(
+                        T.sp[:, a:b], slots, IDENT, bias=-128.0 if mode == "D" else -256.0))
+                if mode == "V":
+                    calls[t, "m" + kh] = ("V", [(t, "G" + kh)], lambda a=a, b=b: wrap(a, a, b))
+                if mode == "F" and not final:
+                    calls[t, "m" + kh] = ("A", [(t, "s" + kh)], lambda a=a, b=b: A.activation(
+                        T.mm[:, a:b], T.sg[:, a:b], IDENT, bias=128.0, scale=-128.0))
+                if mode == "V":
+                    calls[t, "x" + kh] = ("V", [(t, "m" + kh)], lambda a=a, b=b: V.tensor_tensor(
+                        T.xs[:, a:b], T.sp[:, a:b], T.mm[:, a:b], add))
                 if not tail:
-                    calls[t, "a" + kh] = ("P", [(t, "G" + kh)], lambda k=k, qa=qa, qb=qb: part(k, T.Ls, T.sp, qa, qb))
-                    calls[t, "b" + kh] = ("P", [(t, "s" + kh)], lambda k=k, qa=qa, qb=qb: part(k, T.Lg, T.sg, qa, qb))
-
-            if tail and k:
-                banks = [T.X1[:, 0:64 * gp[1][0]], T.RC[:, 0, 0:64 * gp[1][1]]]
-                for h, (qa, qb) in enumerate(cuts(gp[1])):
-                    a, b = base + H + 64 * qa, base + H + 64 * qb
-                    if qb < Q:
-                        calls[t, "X1%d" % h] = ("P", [(t, "s1%d" % h)], lambda h=h, a=a, b=b: x_mm(banks[h], a, b))
-                        calls[t, "x1%d" % h] = ("A", [(t, "X1%d" % h)], lambda h=h, a=a, b=b: x_out(banks[h], a, b))
-                    else:
-                        del calls[t, "s1%d" % h]
-                        calls[t, "m1"] = ("V", [(t, "G1%d" % h)], lambda a=a, b=b: wrap(0, a, b))
-                        calls[t, "x1%d" % h] = ("V", [(t, "m1")], lambda a=a, b=b: V.tensor_tensor(
-                            T.xs[:, a:b], T.sp[:, a:b], T.mm[:, 0:b - a], add))
-            else:
-                a, b = base + H * k, base + H * k + H
-                calls[t, "X%d" % k] = ("P", every("s", [k]), lambda k=k, a=a, b=b: x_mm(X[k][:, 0:H], a, b))
-                calls[t, "x%d" % k] = ("A", [(t, "X%d" % k)], lambda k=k, a=a, b=b: x_out(X[k][:, 0:H], a, b))
+                    val, carry = ("g" if mode in "DA" else "G") + kh, ("G" if mode == "D" else "s") + kh
+                    calls[t, "a" + kh] = ("P", [(t, val)] + opened,
+                                          lambda k=k, qa=qa, qb=qb, mode=mode: part(k, T.Ls, held(mode), qa, qb))
+                    calls[t, "b" + kh] = ("P", [(t, carry)] + opened, lambda k=k, qa=qa, qb=qb, mode=mode: part(
+                        k, T.Lc if mode == "D" else T.Lg, T.sg, qa, qb))
+            for j, (hs, qa, qb, mode) in enumerate(units(t, k)):
+                calls.update(x_calls(t, k, j, hs, base + at[k] + 64 * qa, base + at[k] + 64 * qb, mode))
             if not tail:
                 calls[t, "T%d" % k] = ("V", every("a", [k]) + every("b", [k]), lambda k=k: turn(t, k))
             if not last:
-                i = 2 * (t - 1) + k
+                i = K * (t - 1) + k
                 calls[t, "r%d" % k] = ("g", [(t, "T%d" % k)], lambda k=k, i=i: send(
-                    T.land[:, i, :], T.Tt[:, 2 * t + k, C:2 * C], "r_b%d" % i, "l_%d" % t))
+                    T.land[:, i, 0:C], T.Tt[:, K * t + k, C:2 * C], "r_b%d" % i, "l_%d" % t))
             if not final:
                 calls.update(w_calls(t, k))
-            if t + 2 < M:
-                calls[t, "k%d" % k] = ("P", [(t, "T%d" % k)], lambda k=k: opening(k))
-        if not first:
-            calls.update(u_calls(t, 1, 2, (t, "u")))
+            if not final and role(t + 1) != "tail":
+                calls[t, "k%d" % k] = ("P", [(t, "T%d" % k), ("er", t + 1)], lambda k=k: opening(k, t + 1))
+        xs = every("x")
         if not final:
-            calls.update(s_calls(t, T.xs, base,
-                                 lambda k: every("G", [0, 1]) + [(t, ("m%d" if FUSE[k] else "x%d") % k)]))
-            for k in range(2):
-                if FUSE[k]:
-                    calls[t, "m%d" % k] = ("V", every("G", [k]),
-                                           lambda k=k: wrap(H * k, base + H * k, base + H * k + H))
-            calls.update(u_calls(t + 1, 0, 2 if first else 1, (t, "n")))
-            calls[t, "e"] = ("A", [("er", t + 1)], lambda: shift_e(t + 1))
+            def source(k, qa, qb):
+                hs, fused = under(t, k, qa, qb)
+                if fused:
+                    return [(t, "m%d%d" % (k, h)) for h in hs]
+                return [(t, "x%d%d" % (k, u[0][0])) for u in units(t, k) if set(u[0]) & set(hs)]
+
+            reads = every("G") + every("g")
+            calls.update(s_calls(t, T.xs, base, lambda k, qa, qb: reads + source(k, qa, qb)))
+            calls.update(u_calls(t + 1, 0, K if first else 1, (t, "n")))
+            calls[t, "e"] = ("A", [("er", t + 1)], lambda: shift_e(t + 1, range(K)))
             if not first:
                 calls.update(h_calls(t))
-        left = [] if last else [(t, "r1")]
+        left = [] if last else [(t, "r%d" % (K - 1))]
         if first and t + 2 < M:
             calls[t, "L"] = ("D", left, lambda: load_e(t + 2, t + 3))
-        xs = [(t, "x0"), (t, "x1")]
         if tail:
-            calls[t, "Y0"] = ("D", xs[:1], lambda: store(t * S, t * S + H))
-            calls[t, "Y1"] = ("D", every("x", [1]), lambda: store(t * S + H, (t + 1) * S))
+            calls[t, "Y0"] = ("D", every("x", range(K - 1)), lambda: store(t * S, t * S + at[-1]))
+            end = S - 64 * GP["tail"][-1][-1] * LAST
+            calls[t, "Y1"] = ("D", sorted(every("x", [K - 1]))[:-1 if LAST else None],
+                              lambda: store(t * S + at[-1], t * S + end))
+            if LAST:
+                calls[t, "Y2"] = ("D", every("x", [K - 1]), lambda: store(t * S + end, (t + 1) * S))
+        elif ADD:
+            if rank >= n - 2 or final:
+                a = t * S if rank >= n - 2 else S
+                calls[t, "Y0"] = ("D", left + xs + every("G"), lambda: store(a, (t + 1) * S, "d_y%d" % t))
+            if last or final:
+                a0, b0 = (t, t + 1) if last else (1, t)
+                stored = [(i, "Y0") for i in range(a0, b0)] if rank >= n - 2 else [(t, "Y0")]
+                calls[t, "Z0"] = ("g", stored + every("m") + ["zero"] + ([] if last else [(t - 1, "e")]), lambda: sig(g.dma_start(
+                    T.y[:, a0 * S:b0 * S], T.mm[:, (a0 - 1) * S:(b0 - 1) * S], accum_op=add, max_dma_last_dim=2 * S),
+                    "g_y", 16))
+            if first and final:
+                calls[t, "Y1"] = ("D", [], store0)
         elif rank >= n - 2:
             calls[t, "Y0"] = ("D", left + xs, lambda: store(t * S, (t + 1) * S))
         elif final:
             calls[t, "Y0"] = ("D", left + xs, lambda: store(S, M * S))
             if first:
                 calls[t, "Y1"] = ("D", [], store0)
+        if not first:
+            for k in range(1, K):
+                calls.update(u_calls(t, k, k + 1, (t, "u%d" % k)))
         emit({"V": named(t, V_TAIL if tail else V_FINAL if final else V_FIRST if first else V_NEXT),
-              "A": named(t, A_TAIL if tail else A_STEP),
-              "P": named(t, P_TAIL if tail else P_STEP), "g": named(t, "r0 r1"), "D": named(t, "L Y0 Y1")}, calls)
+              "A": named(t, A_TAIL if tail else A_FINAL if final else A_FIRST if first else A_STEP),
+              "P": named(t, P_TAIL if tail else P_FINAL if final else P_FIRST if first else P_STEP),
+              "g": named(t, "r0 r1 Z0"), "D": named(t, "L Y0 Y1 Y2")}, calls)
 
     for name in cnt:
         if done.get(name, 0) < cnt[name]:

from concourse.mybir import AluOpType, ActivationFunctionType

W, S, M = 8192, 768, 5
BIG = float(2 ** 20)
MAGIC = 1.5 * 2 ** 26

PART = (6, 6)
GP = {"first": ((2, 2, 2), (2, 2, 2)), "next": ((2, 2, 2), (2, 2, 2)), "final": ((2, 2, 2), (2, 2, 2)),
      "tail": ((2, 2, 2), (2, 2, 2))}
MODE = {"first": ("FFD", "FFD"), "next": ("FFD", "FFD"), "final": ("SSD", "SSD"), "tail": ("SSS", "SSV")}
SP = ((2, 2, 2), (4, 2))
TB = (6, 12)
ROUND = 1
V_ZERO = "Tc L T0 w01 T1 S00 w10 S01 w11 n1 S02 n2 S10 S11"
V_ZERO_NEXT = "Tc L T0 T1 w10 w01 w11 S00 S01 S02 S10 S11 n0 n2"
V_FIRST = "G00 G01 G02 G11 G10 G12 T0 w00 w01 T1 S00 w10 S01 n1 w11 S02 n2 S11 S10"
V_NEXT = "G00 u10 u11 G01 u12 G02 G10 G11 G12 T0 w00 w01 T1 S00 w10 S01 w11 S02 S10 n0 S11 n2"
V_FINAL = "G00 u10 u11 G01 u12 G02 G10 G11 G12 T0 T1"
V_TAIL = "G00 u10 u11 G01 u12 G02 G10 G11 G12 m12 x12"
A_FIRST = "g02 g12 s00 s01 s11 s10 m00 m01 e x12 x02 m10 n0 m11"
A_STEP = "g02 s00 s01 g12 s10 s11 m01 f0 m00 m10 m11 h0 x02 f1 x12 e h1"
A_FINAL = "g02 s00 s01 g12 s10 s11 x10 x12 x02 x00"
A_TAIL = "s00 s01 s02 x00 s10 s11 x01 x02 x10 x11"
P_FIRST = "a00 a02 a01 b02 b00 b01 a12 a10 b11 b12 a11 b10 X02 X12 k1 k0"
P_STEP = "a00 a02 a01 b00 b02 b01 a12 a10 a11 b10 b11 b12 d0 X02 X12 k0 o0 d1 k1 n1"
P_FINAL = "a00 a02 a01 b00 b02 b01 a10 a11 a12 b12 b10 b11 X10 X02 X00 X12"
P_TAIL = "X00 X01 X02 X10 X11"
BYPE = (1, 1)
EARLY = 2
STEP = 1
ADD = 1
SPLIT = "PP"
LAST = 0

NK = 4
SCRATCH = {
    "tb": ("sbuf", [128, W], "bfloat16"),
    "er": ("sbuf", [128, M * S], "bfloat16"),
    "ep": ("sbuf", [128, 4 * S], "bfloat16"),
    "sp": ("sbuf", [128, 4 * S], "bfloat16"),
    "sg": ("sbuf", [128, 4 * S], "bfloat16"),
    "xs": ("sbuf", [128, 4 * S], "bfloat16"),
    "mm": ("sbuf", [128, 4 * S], "bfloat16"),
    "hws": ("sbuf", [128, 16], "bfloat16"),
    "Ls": ("sbuf", [128, 2, 160], "bfloat16"),
    "Lg": ("sbuf", [128, 2, 160], "bfloat16"),
    "Lc": ("sbuf", [128, 2, 160], "bfloat16"),
    "Gp": ("sbuf", [128, 2, 4], "bfloat16"),
    "one8": ("sbuf", [128, 2, 4], "bfloat16"),
    "ones": ("sbuf", [128, 128], "bfloat16"),
    "idf": ("sbuf", [128, 128], "float32"),
    "idm": ("sbuf", [128, 128], "bfloat16"),
    "idp": ("sbuf", [128, 128], "bfloat16"),
    "idn": ("sbuf", [128, 128], "bfloat16"),
    "idh": ("sbuf", [128, 128], "bfloat16"),
    "c128": ("sbuf", [128, 32], "bfloat16"),
    "Kc": ("sbuf", [128, NK, 4, 32], "bfloat16"),
    "Kr": ("sbuf", [128, 2, 64], "bfloat16"),
    "Tt": ("sbuf", [128, NK * M, 128], "float32"),
    "Tc": ("sbuf", [128, 32], "float32"),
    "cvin": ("sbuf", [128, 8], "float32"),
    "col": ("sbuf", [128, 8], "float32"),
    "land": ("sbuf", [128, 4 * NK, 32], "float32"),
    "ru": ("sbuf", [128, 4 * NK, 32], "bfloat16"),
    "du": ("sbuf", [128, 4 * NK, 32], "float32"),
    "h1": ("sbuf", [128, 4 * NK, 32], "float32"),
    "h2": ("sbuf", [128, 4 * NK, 32], "float32"),
    "hr": ("sbuf", [128, 4 * NK, 32], "bfloat16"),
    "ha": ("sbuf", [128, 4 * NK, 32], "float32"),
    "offu": ("sbuf", [128, 4 * NK, 32], "uint16"),
    "rw": ("sbuf", [128, 4 * NK, 32], "float32"),
    "offw": ("sbuf", [128, 4 * NK, 32], "uint16"),
    "PS": ("psum", [128, 8, 8, 64], "float32"),
}
SEMAPHORES = (
    ["V", "A", "P", "g", "d_hw", "d_e0", "d_e1", "d_f1", "d_e2", "d_e3", "d_e4", "d_y", "d_y1", "d_y2", "d_y3", "d_y4", "g_y"] + ["d_t%d" % i for i in range(6)]
    + ["r_c", "l_c"] + ["r_b%d" % i for i in range(4 * NK)] + ["l_%d" % t for t in range(1, M)]
)


def cuts(parts):
    return [(sum(parts[:i]), sum(parts[:i + 1])) for i in range(len(parts))]


def rank_program(g, core, T, topo):
    rank = T.rank_of(core)
    if rank is None:
        return
    n = len(T.cores)
    first, last = rank == 0, rank == n - 1
    V, A, P, D = g.vector, g.scalar, g.tensor, g.sync
    queue = {"V": V, "A": A, "P": P, "D": D, "g": g}
    add, sub, mul = AluOpType.add, AluOpType.subtract, AluOpType.mult
    IDENT, SIGN = ActivationFunctionType.Identity, ActivationFunctionType.Sign
    K, Q = len(PART), max(PART)
    C = 4 * Q
    at = [64 * a for a, _ in cuts(PART)]
    cnt, seen, done = {}, {}, {}

    def sig(ins, name, k=1):
        ins.then_inc(T.sem[name], k)
        return owe(name, k)

    def owe(name, k):
        cnt[name] = cnt.get(name, 0) + k
        return (name, cnt[name])

    def wait(qn, *toks):
        most = {}
        for name, k in toks:
            most[name] = max(most.get(name, 0), k)
        for name, k in most.items():
            if seen.get((qn, name), 0) < k:
                queue[qn].wait_ge(T.sem[name], k)
                seen[(qn, name)] = k
                done[name] = max(done.get(name, 0), k)

    tok = {}

    def emit(orders, calls):
        todo = {q: [c for c in order if c in calls and calls[c][0] == q] for q, order in orders.items()}
        assert sum(len(v) for v in todo.values()) == len(calls)
        while any(todo.values()):
            moved = False
            for q, names in todo.items():
                while names and all(d in tok for d in calls[names[0]][1]):
                    name = names.pop(0)
                    wait(q, *[tok[d] for d in calls[name][1]])
                    ins = calls[name][2]()
                    tok[name] = ins if isinstance(ins, tuple) else sig(ins, q)
                    moved = True
            assert moved, todo

    if not last:
        nxt = T.cores[rank + 1]
        rid, pid, _ = topo.addr(nxt)
        some = topo.engines(core, nxt)[::STEP]
        omask, oeng = sum(1 << e for e in some), len(some)
    if not first:
        ieng = len(topo.engines(T.cores[rank - 1], core)[::STEP])
        tok["cv"] = owe("r_c", ieng)
        for i in range(4 * K):
            tok["land", i] = owe("r_b%d" % i, ieng)

    def send(dst, src, rsem, lsem):
        g.remote_dma(dst, src, T.sem[rsem], T.sem[lsem], pid, rid, omask)
        return owe(lsem, oeng)

    d_hw = sig(A.dma_start(T.hws[:, 0:3], T.hw[:]), "d_hw", 16)

    def load_e(t0, t1):
        d = sig(D.dma_start(T.er[:, t0 * S:t1 * S], T.res[:, t0 * S:t1 * S]), "d_e%d" % t0, 16)
        for t in range(t0, t1):
            tok["er", t] = d
        return d

    def load_t(i, a, b):
        tok["tb", i] = sig(D.dma_start(T.tb[:, a:b], T.tab[:, a:b]), "d_t%d" % i, 16)

    load_e(0, 1)
    for i, b in enumerate(TB):
        load_t(i, 512 * (TB[i - 1] if i else 0), 512 * b)
    def load_first(k0, k1, name):
        a, b = S + at[k0], S + (at + [S])[k1]
        d = sig(D.dma_start(T.er[:, a:b], T.res[:, a:b]), name, 16)
        for k in range(k0, k1):
            tok["er", 1, k] = d

    load_first(0, EARLY, "d_e1")
    load_t(len(TB), 8 * S, W)
    if EARLY < K:
        load_first(EARLY, K, "d_f1")
    load_e(2, 3 if first else M)

    def store(a, b, name="d_y"):
        return sig(D.dma_start(T.y[:, a:b], T.xs[:, a - S:b - S]), name, 16)

    def store0():
        wait("D", tok["er", 0])
        return sig(D.dma_start(T.y[:, 0:S], T.er[:, 0:S]), "d_y", 16)

    if not first:
        store0()

    v_one8 = sig(V.memset(T.one8[:], 1.0), "V")
    v_kc = sig(V.memset(T.Kc[0:64], 0.0), "V")
    g_kr = sig(g.iota(T.Kr[0:32], [[0, 2], [8, 64]], 0, 0, allow_small_or_imprecise_dtypes=True), "g")
    wait("g", v_one8)
    g0 = sig(g.affine_select(T.Gp[:], T.one8[:], [[-16, 2], [-32, 4]], AluOpType.is_ge, 0.0, 0, 1), "g")
    wait("g", g0)
    g1 = sig(g.affine_select(T.Gp[:], T.Gp[:], [[16, 2], [32, 4]], AluOpType.is_ge, 0.0, 15, -1), "g")
    V.memset(T.Ls[:], 0.0)
    v_ones = sig(V.memset(T.ones[:], 1.0), "V")
    V.memset(T.Kr[32:64], 1.0)
    wait("V", v_kc)
    V.memset(T.Kc[32:33, 0:K, :, 2 * Q:3 * Q], -3.5)
    V.memset(T.Kc[0:1, 0:K, :, 3 * Q:4 * Q], 1.0)
    for k in range(K):
        step = SP[k][0] if len(set(SP[k])) == 1 else Q
        for a, b in cuts(SP[k])[:1 if step < Q else None]:
            for q in range(a + 1, b):
                V.memset(T.Kc[32:33, k, :, 3 * Q + q:4 * Q:step], 512.0 * (q - a))
    V.memset(T.Kc[32:33, K, :, 2 * Q:3 * Q], MAGIC)
    v_z = sig(V.memset(T.Kc[32:33, K + 1, :, 2 * Q:3 * Q], -MAGIC), "V")
    v_l = sig(V.memset(T.c128[:], 128.0), "V")
    wait("g", v_ones)
    for o, c in ((T.idp, 1.0), (T.idf, 1.0)):
        tok["id"] = sig(g.affine_select(o[:], T.ones[:], [[-1, 128]], AluOpType.is_equal, 0.0, 0, 1), "g")

    def weights(L, kinds, scale):
        for kind in kinds:
            o, w = Q - 1 + Q * kind, min(kind, 2)
            ins = V.tensor_scalar(L[:, :, o:o + 128:32], T.Gp[:], T.hws[:, w:w + 1], scale, mul, mul)
        return ins

    wait("V", v_ones, g1, d_hw)
    tok["Ls"] = sig(weights(T.Ls, (2, 3, 0, 1), 1.0), "V")
    V.memset(T.Lg[:], 0.0)
    tok["L0"] = sig(V.memset(T.Lc[:], 0.0), "V")
    wait("A", tok["id"])
    for o, c in ((T.idm, -1.0), (T.idn, -128.0), (T.idh, -256.0)):
        tok["ids"] = sig(A.activation(o[:], T.idp[:], IDENT, scale=c), "A")

    def role(t):
        return ("tail" if last else "final") if t == M - 1 else "first" if first else "next"

    def pieces(t, k):
        return [(h, qa, qb, MODE[role(t)][k][h]) for h, (qa, qb) in enumerate(cuts(GP[role(t)][k]))]

    def opening(k, t):
        ins = P.matmul(T.PS[:, k, 0:2, :], T.Kc[0:64, k], T.Kr[0:64], True, False)
        for h, qa, qb, mode in pieces(t, k) if t else []:
            if mode in "DA":
                ins = sums(k, T.Ls, T.er, t * S + at[k], qa, qb, False)
        return ins

    def sums(k, L, src, base, q0, q1, stop):
        for q in range(q0, q1):
            for par in range(2):
                ins = P.matmul(T.PS[:, k, par, :], L[:, par, Q - 1 - q:Q + 127 - q],
                               src[:, base + 64 * q:base + 64 * q + 64], False, stop and q == q1 - 1 and par == 1)
        return ins

    def turn(t, k):
        for b in range(4):
            ins = V.transpose(T.Tt[:, K * t + k, b:128:4], T.PS[:, k, 0:2, 16 * b:16 * b + 16])
        return ins

    def w_calls(t, k):
        i = K * t + k
        if t == 0 and k < ROUND:
            return {(t, "w%d1" % k): ("V", [(t, "T%d" % k)], lambda: V.tensor_tensor(
                T.offw[:, i, 0:C], T.Tt[:, i, 3 * C:4 * C], T.Tt[:, i, 2 * C:3 * C], sub))}
        return {
            (t, "w%d0" % k): ("V", [(t, "T%d" % k)], lambda: V.tensor_scalar(
                T.rw[:, i, 0:C], T.Tt[:, i, 2 * C:3 * C], MAGIC, MAGIC, add, sub)),
            (t, "w%d1" % k): ("V", [(t, "w%d0" % k)], lambda: V.tensor_tensor(
                T.offw[:, i, 0:C], T.Tt[:, i, 3 * C:4 * C], T.rw[:, i, 0:C], sub)),
        }

    def u_calls(t, k0, k1, name):
        a, b = K * (t - 1) + k0, K * (t - 1) + k1
        s, c = name
        hr, ha = T.hr[:, a:b, 0:C], T.ha[:, a:b, 0:C]
        if first:
            deps = [(t - 1, "T%d" % k) for k in range(K)] + ["col"]
            lo, hi = (BIG + W - 4095.5, BIG + W) if t == 1 else (T.col[:, 0:1], T.col[:, 1:2])
            calls = {(s, c + "0"): ("A", deps, lambda: A.activation(hr, T.Tt[:, a:b, 0:C], IDENT, bias=lo)),
                     (s, c + "1"): ("V", deps, lambda: V.tensor_scalar(ha, T.Tt[:, a:b, 0:C], hi, None, add))}
        else:
            deps = [(t - 1, "h%d" % k0 if SPLIT else "h"), ("land", a)]
            land = T.land[:, a:b, 0:C]
            calls = {(s, c + "0"): ("V", deps, lambda: V.tensor_tensor(hr, T.h1[:, a:b, 0:C], land, add)),
                     (s, c + "1"): ("V", deps, lambda: V.tensor_tensor(ha, T.h2[:, a:b, 0:C], land, add))}
            if k0 < BYPE[1]:
                ha = T.PS[:, 7 - k0, 0, 0:C]
                calls[s, c + "1"] = ("P", [(t - 1, "o%d" % k0), ("land", a)],
                                     lambda: P.matmul(ha, T.idf[:], T.land[:, a, 0:C], False, True))
        calls[s, c + "2"] = ("V", [(s, c + "0"), (s, c + "1")], lambda: V.tensor_tensor(T.offu[:, a:b, 0:C], ha, hr, sub))
        return calls

    def held(mode):
        return T.xs if mode == "F" and ADD else T.sp

    def under(t, k, qa, qb):
        over = [(h, mode) for h, pa, pb, mode in pieces(t, k) if pa < qb and qa < pb]
        return [h for h, _ in over], all(mode == "F" for _, mode in over)

    def s_calls(t, src, base, deps):
        calls = {}
        for k in range(K):
            for i, (qa, qb) in enumerate(cuts(SP[k])):
                def scatter(k=k, qa=qa, qb=qb):
                    a, b = at[k] + 64 * qa, at[k] + 64 * qb
                    win = T.tb[:, 8 * a:8 * b].indirect(T.offw[:, K * t + k, 4 * qa:4 * qb])
                    if t and under(t, k, qa, qb)[1]:
                        return V.tensor_tensor(win, held("F")[:, base + a:base + b], T.mm[:, base + a:base + b], add)
                    return V.tensor_copy(win, src[:, base + a:base + b])
                calls[t, "S%d%d" % (k, i)] = ("V", [(t, "w%d1" % k)] + deps(k, qa, qb), scatter)
        return calls

    free = {}

    def units(t, k):
        out = []
        for h, qa, qb, mode in pieces(t, k):
            if out and out[-1][3] == mode != "A" and role(t) != "tail":
                out[-1][0].append(h)
                out[-1][2] = qb
            elif mode != "V" and not (mode == "F" and ADD):
                out.append([[h], qa, qb, mode])
        return out

    def x_calls(t, k, j, hs, a, b, mode):
        i = K + j + sum(len(units(t, p)) for p in range(k))
        assert i < 8 - max(BYPE) or first or role(t) == "tail"
        bank, kh, calls = T.PS[:, i, 0:(b - a) // 64, :], "%d%d" % (k, hs[0]), {}

        def x_mm(whole):
            if mode in "DA":
                P.matmul(bank, T.idp[:], T.er[:, S + a:S + b], True, False)
            ins = P.matmul(bank, T.idp[:], T.sp[:, a:b], mode not in "DA", not whole)
            return P.matmul(bank, T.idh[:] if mode == "D" else T.idn[:], T.sg[:, a:b], False, True) if whole else ins

        if mode == "A":
            calls[t, "z" + kh] = ("P", free.get(i, []) + [("er", t) if t > 1 else ("er", t, k)],
                                  lambda: P.matmul(bank, T.idp[:], T.er[:, S + a:S + b], True, False))
            calls[t, "Z" + kh] = ("P", [(t, "g" + kh)], lambda: P.matmul(bank, T.idp[:], T.sp[:, a:b], False, True))
            calls[t, "s" + kh] = ("A", [(t, "Z" + kh)], lambda: A.activation(T.sg[:, a:b], bank, SIGN, bias=0.5))
        deps = [(t, "%s%d%d" % (c, k, h)) for h in hs for c in ("gG" if mode == "D" else "s")]
        if i >= 6 and not first:
            deps.append((t, "u12"))
        calls[t, "X" + kh] = ("P", deps + free.get(i, []), lambda: x_mm(True))
        calls[t, "x" + kh] = ("A", [(t, "X" + kh)], lambda: A.activation(T.xs[:, a:b], bank, IDENT, bias=128.0))
        free[i] = [(t, "x" + kh)]
        return calls

    def wrap(o, a, b):
        return V.tensor_scalar(T.mm[:, o:o + b - a], T.sp[:, a:b], 0.0, 256.0, AluOpType.is_lt, mul)

    def shift_e(t, ks):
        spans = []
        for k in ks:
            for h, qa, qb, mode in pieces(t, k):
                a, b = at[k] + 64 * qa, at[k] + 64 * qb
                if mode != "A" and spans and spans[-1][1:] == [a, mode == "D"]:
                    spans[-1][1] = b
                elif mode != "A":
                    spans.append([a, b, mode == "D"])
        for a, b, dual in spans:
            ins = A.activation(T.ep[:, (t - 1) * S + a:(t - 1) * S + b], T.er[:, t * S + a:t * S + b],
                               IDENT, bias=255.0 if dual else -256.0, scale=-1.0 if dual else 1.0)
        return ins

    def h_calls(t):
        if not SPLIT:
            return h_all(t)
        calls = {}
        up, lo, hi = ((T.col[:, 0:1], T.col[:, 3:4], T.col[:, 4:5]) if t else (BIG + 0.5, T.col[:, 1:2], T.col[:, 2:3]))
        for k in range(K):
            i = K * t + k
            u, ru = T.Tt[:, i, 0:C], T.ru[:, i, 0:C]
            du = T.PS[:, 7 - k, 0, 0:C] if SPLIT[k] == "P" else T.du[:, i, 0:C]

            def minus(u=u, ru=ru, du=du, k=k):
                if SPLIT[k] == "V":
                    return V.tensor_tensor(du, u, ru, sub)
                P.matmul(du, T.idf[:], u, True, False)
                return P.matmul(du, T.idm[:], ru, False, True)

            def both(i=i, du=du):
                A.activation(T.h1[:, i, 0:C], du, IDENT, bias=lo)
                return A.activation(T.h2[:, i, 0:C], du, IDENT, bias=hi)

            calls[t, "f%d" % k] = ("A", [(t, "T%d" % k), "col"], lambda u=u, ru=ru: A.activation(ru, u, IDENT, bias=up))
            calls[t, "d%d" % k] = (SPLIT[k], [(t, "f%d" % k), "ids", "Tc"], minus)
            calls[t, "h%d" % k] = ("A", [(t, "d%d" % k), "col2" if t else "col1"], both)
            if k < BYPE[1]:
                calls[t, "o%d" % k] = ("P", [(t, "h%d" % k)], lambda k=k, i=i: P.matmul(
                    T.PS[:, 7 - k, 0, 0:C], T.idf[:], T.h2[:, i, 0:C], True, False))
        return calls

    def h_all(t):
        a, b = K * t, K * t + K
        u, du = T.Tt[:, a:b, 0:C], T.du[:, a:b, 0:C]
        up, lo, hi = ((T.col[:, 0:1], T.col[:, 3:4], T.col[:, 4:5]) if t else (BIG + 0.5, T.col[:, 1:2], T.col[:, 2:3]))

        def both():
            A.activation(T.h1[:, a:b, 0:C], du, IDENT, bias=lo)
            return A.activation(T.h2[:, a:b, 0:C], du, IDENT, bias=hi)

        calls = {(t, "r"): ("A", [(t, "T%d" % k) for k in range(K)] + ["col"],
                            lambda: A.activation(T.ru[:, a:b, 0:C], u, IDENT, bias=up)),
                 (t, "d"): ("V", [(t, "r")], lambda: V.tensor_tensor(du, u, T.ru[:, a:b, 0:C], sub)),
                 (t, "h"): ("A", [(t, "d"), "col2"], both)}
        if BYPE[0]:
            du = T.PS[:, 7, 0:K, 0:C]

            def minus():
                P.matmul(du, T.idf[:], u, True, False)
                return P.matmul(du, T.idm[:], T.ru[:, a:b, 0:C], False, True)

            calls[t, "d"] = ("P", [(t, "r"), "ids", "Tc"], minus)
        for k in range(BYPE[1]):
            calls[t, "o%d" % k] = ("P", [(t, "h")], lambda k=k: P.matmul(
                T.PS[:, 7 - k, 0, 0:C], T.idf[:], T.h2[:, a + k, 0:C], True, False))
        return calls

    if ADD:
        wait("A", tok["er", 0])
        for t in range(1, M - 1):
            for k in range(K):
                for hs, qa, qb, mode in units(t, k):
                    a, b = (t - 1) * S + at[k] + 64 * qa, (t - 1) * S + at[k] + 64 * qb
                    tok["zero"] = sig(A.activation(T.mm[:, a:b], T.er[:, 0:b - a], IDENT, scale=0.0), "A")

    def named(t, order):
        return [c if c in ("Tc", "pc", "cs", "col", "col1", "col2") else (t, c) for c in order.split()]

    calls = {(0, "e%d" % k): ("A", [("er", 1, k)], lambda k=k: shift_e(1, [k])) for k in range(EARLY if first else K)}
    wait("P", v_z, g_kr)
    for k in range(K):
        opening(k, 0)

        def zero(k=k):
            ins = sums(k, T.Ls, T.er, at[k], 0, PART[k], k >= ROUND)
            for i in range(2 * (k < ROUND)):
                ins = P.matmul(T.PS[:, k, 0:2, :], T.Kc[0:64, K + i], T.Kr[0:64], False, i == 1)
            return ins

        calls[0, "b%d" % k] = ("P", ["Ls", ("er", 0)], zero)
        calls[0, "T%d" % k] = ("V", [(0, "b%d" % k)], lambda k=k: turn(0, k))
        if k < EARLY or not first:
            calls[0, "k%d" % k] = ("P", [(0, "T%d" % k), ("er", 1, k)], lambda k=k: opening(k, 1))
        calls.update(w_calls(0, k))

    def const_sums():
        for par in range(2):
            ins = P.matmul(T.PS[:, 6 + par, 0, 0:16], T.Ls[:, par, Q - 1:Q + 127], T.c128[:, 0:16], True, True)
        return ins

    def column(i, src, bias):
        return A.activation(T.col[:, i:i + 1], src, IDENT, bias=bias)

    cu, cv = T.Tc[:, 0:1], T.cvin[:, 0:1]
    tok["c128"] = v_l
    calls[0, "L"] = ("V", ["L0"], lambda: [weights(T.Lg, (0, 1), -128.0), weights(T.Lc, (0, 1), -256.0)][1])
    calls["pc"] = ("P", ["c128", "Ls"], const_sums)
    calls["Tc"] = ("V", ["pc"], lambda: V.transpose(T.Tc[:], T.PS[:, 6:8, 0, 0:16]))
    free[6] = free[7] = ["Tc"]
    calls.update(s_calls(0, T.er, 0, lambda k, qa, qb: [("tb", i) for i in range(len(TB))
                                                         if (TB[i - 1] if i else 0) < at[k] // 64 + qb]))
    if not last:
        calls["cs"] = ("g", ["Tc"], lambda: send(T.cvin[:, 0:1], T.Tc[:, Q:Q + 1], "r_c", "l_c"))
    if first:
        tok["col"] = tok["Ls"]
        calls.update(u_calls(1, 0, K, (0, "n")))
        calls["col1"] = ("A", ["Tc"], lambda: [column(0, cu, BIG + W - 4095.5), column(1, cu, BIG + W)][1])
    else:
        calls.update(u_calls(1, 0, 1, (0, "n")))
        calls.update(h_calls(0))
        calls["col"] = ("A", ["Tc"], lambda: column(0, cu, BIG + 0.5))
        calls["col1"] = ("A", ["cv"], lambda: [column(1, cv, 2 * BIG + W - 4095.5), column(2, cv, 2 * BIG + W)][1])
        calls["col2"] = ("A", ["col1"], lambda: [column(3, cu, T.col[:, 1:2]), column(4, cu, T.col[:, 2:3])][1])
    emit({"P": named(0, "pc b0 b1 k0 k1 d d0 d1 o0 o1 n1"), "V": named(0, V_ZERO if first else V_ZERO_NEXT), "g": ["cs"],
          "A": named(0, "n0 col r f0 f1 e0 e1 col1 h0 h1 col2 h")}, calls)
    if first:
        tok["col"] = tok["col1"]
    wait("P", tok[0, "L"], tok["ids"])

    for t in range(1, M):
        final = t == M - 1
        tail = final and last
        base = (t - 1) * S
        calls = {}
        table = [(t - 1, "S%d%d" % (k, i)) for k in range(K) for i in range(len(SP[k]))] + [("tb", len(TB))]
        every = lambda c, ks=range(K): [x for x in calls if x[1][0] == c and int(x[1][1]) in ks]
        issued = {k: [] for k in range(K)}

        def part(k, L, src, qa, qb):
            issued[k].append(qa)
            return sums(k, L, src, base + at[k], qa, qb, len(issued[k]) == 2 * len(pieces(t, k)))

        for k in range(K):
            shifted, opened = (t - 1, "e" if t > 1 else "e%d" % k), []
            if first and t == 1 and k >= EARLY:
                shifted, opened = (t, "E%d" % k), [(t, "O%d" % k)]
                calls[shifted] = ("A", [("er", 1, k)], lambda k=k: shift_e(1, [k]))
                calls[opened[0]] = ("P", [(0, "T%d" % k), ("er", 1, k)], lambda k=k: opening(k, 1))
            for h, qa, qb, mode in pieces(t, k):
                a, b = base + at[k] + 64 * qa, base + at[k] + 64 * qb
                kh = "%d%d" % (k, h)
                ready = table + [(t - 1, "n2") if first or k == 0 else (t, "u%d2" % k)]
                slots = T.tb[:, 0:W].indirect(T.offu[:, K * (t - 1) + k, 4 * qa:4 * qb])
                if mode != "A":
                    out, op = (T.sg, AluOpType.is_gt) if mode == "D" else (held(mode), add)
                    calls[t, "G" + kh] = ("V", ready + [shifted], lambda a=a, b=b, slots=slots, out=out, op=op:
                                          V.tensor_tensor(out[:, a:b], slots, T.ep[:, a:b], op))
                if mode in "SF":
                    calls[t, "s" + kh] = ("A", [(t, "G" + kh)], lambda a=a, b=b, mode=mode: A.activation(
                        T.sg[:, a:b], held(mode)[:, a:b], SIGN, bias=0.5))
                if mode in "DA":
                    calls[t, "g" + kh] = ("A", ready, lambda a=a, b=b, slots=slots, mode=mode: A.activation(
                        T.sp[:, a:b], slots, IDENT, bias=-128.0 if mode == "D" else -256.0))
                if mode == "V":
                    calls[t, "m" + kh] = ("V", [(t, "G" + kh)], lambda a=a, b=b: wrap(a, a, b))
                if mode == "F" and not final:
                    calls[t, "m" + kh] = ("A", [(t, "s" + kh)], lambda a=a, b=b: A.activation(
                        T.mm[:, a:b], T.sg[:, a:b], IDENT, bias=128.0, scale=-128.0))
                if mode == "V":
                    calls[t, "x" + kh] = ("V", [(t, "m" + kh)], lambda a=a, b=b: V.tensor_tensor(
                        T.xs[:, a:b], T.sp[:, a:b], T.mm[:, a:b], add))
                if not tail:
                    val, carry = ("g" if mode in "DA" else "G") + kh, ("G" if mode == "D" else "s") + kh
                    calls[t, "a" + kh] = ("P", [(t, val)] + opened,
                                          lambda k=k, qa=qa, qb=qb, mode=mode: part(k, T.Ls, held(mode), qa, qb))
                    calls[t, "b" + kh] = ("P", [(t, carry)] + opened, lambda k=k, qa=qa, qb=qb, mode=mode: part(
                        k, T.Lc if mode == "D" else T.Lg, T.sg, qa, qb))
            for j, (hs, qa, qb, mode) in enumerate(units(t, k)):
                calls.update(x_calls(t, k, j, hs, base + at[k] + 64 * qa, base + at[k] + 64 * qb, mode))
            if not tail:
                calls[t, "T%d" % k] = ("V", every("a", [k]) + every("b", [k]), lambda k=k: turn(t, k))
            if not last:
                i = K * (t - 1) + k
                calls[t, "r%d" % k] = ("g", [(t, "T%d" % k)], lambda k=k, i=i: send(
                    T.land[:, i, 0:C], T.Tt[:, K * t + k, C:2 * C], "r_b%d" % i, "l_%d" % t))
            if not final:
                calls.update(w_calls(t, k))
            if not final and role(t + 1) != "tail":
                calls[t, "k%d" % k] = ("P", [(t, "T%d" % k), ("er", t + 1)], lambda k=k: opening(k, t + 1))
        xs = every("x")
        if not final:
            def source(k, qa, qb):
                hs, fused = under(t, k, qa, qb)
                if fused:
                    return [(t, "m%d%d" % (k, h)) for h in hs]
                return [(t, "x%d%d" % (k, u[0][0])) for u in units(t, k) if set(u[0]) & set(hs)]

            reads = every("G") + every("g")
            calls.update(s_calls(t, T.xs, base, lambda k, qa, qb: reads + source(k, qa, qb)))
            calls.update(u_calls(t + 1, 0, K if first else 1, (t, "n")))
            calls[t, "e"] = ("A", [("er", t + 1)], lambda: shift_e(t + 1, range(K)))
            if not first:
                calls.update(h_calls(t))
        left = [] if last else [(t, "r%d" % (K - 1))]
        if first and t + 2 < M:
            calls[t, "L"] = ("D", left, lambda: load_e(t + 2, t + 3))
        if tail:
            calls[t, "Y0"] = ("D", every("x", range(K - 1)), lambda: store(t * S, t * S + at[-1]))
            end = S - 64 * GP["tail"][-1][-1] * LAST
            calls[t, "Y1"] = ("D", sorted(every("x", [K - 1]))[:-1 if LAST else None],
                              lambda: store(t * S + at[-1], t * S + end))
            if LAST:
                calls[t, "Y2"] = ("D", every("x", [K - 1]), lambda: store(t * S + end, (t + 1) * S))
        elif ADD:
            if rank >= n - 2 or final:
                a = t * S if rank >= n - 2 else S
                calls[t, "Y0"] = ("D", left + xs + every("G"), lambda: store(a, (t + 1) * S, "d_y%d" % t))
            if last or final:
                a0, b0 = (t, t + 1) if last else (1, t)
                stored = [(i, "Y0") for i in range(a0, b0)] if rank >= n - 2 else [(t, "Y0")]
                calls[t, "Z0"] = ("g", stored + every("m") + ["zero"] + ([] if last else [(t - 1, "e")]), lambda: sig(g.dma_start(
                    T.y[:, a0 * S:b0 * S], T.mm[:, (a0 - 1) * S:(b0 - 1) * S], accum_op=add, max_dma_last_dim=2 * S),
                    "g_y", 16))
            if first and final:
                calls[t, "Y1"] = ("D", [], store0)
        elif rank >= n - 2:
            calls[t, "Y0"] = ("D", left + xs, lambda: store(t * S, (t + 1) * S))
        elif final:
            calls[t, "Y0"] = ("D", left + xs, lambda: store(S, M * S))
            if first:
                calls[t, "Y1"] = ("D", [], store0)
        if not first:
            for k in range(1, K):
                calls.update(u_calls(t, k, k + 1, (t, "u%d" % k)))
        emit({"V": named(t, V_TAIL if tail else V_FINAL if final else V_FIRST if first else V_NEXT),
              "A": named(t, A_TAIL if tail else A_FINAL if final else A_FIRST if first else A_STEP),
              "P": named(t, P_TAIL if tail else P_FINAL if final else P_FIRST if first else P_STEP),
              "g": named(t, "r0 r1 Z0"), "D": named(t, "L Y0 Y1 Y2")}, calls)

    for name in cnt:
        if done.get(name, 0) < cnt[name]:
            wait("g" if name[0] == "l" else "D", (name, cnt[name]))
